import numpy as np
import ml_dtypes


def mxq(x, axis, fmt="e4m3"):
    dtype, down = {"e4m3": (ml_dtypes.float8_e4m3fn, 7), "e5m2": (ml_dtypes.float8_e5m2, 14)}[fmt]
    v = np.moveaxis(np.asarray(x, np.float32).astype(ml_dtypes.bfloat16).astype(np.float64), axis, -1)
    blocks = v.reshape(v.shape[:-1] + (-1, 32))
    amax = np.abs(blocks).max(-1, keepdims=True)
    byte = np.maximum(np.where(amax > 0, np.frexp(amax)[1] - 1 + 127, 0) - down, 1)
    scale = np.exp2(byte - 127.0)
    codes = (blocks / scale).astype(np.float32).astype(dtype).astype(np.float64)
    return np.moveaxis((codes * scale).reshape(v.shape), -1, axis)


WIDE = False


def mx_kscale(k):
    if not WIDE:
        return np.ones(k)
    levels = np.array([10, -10, 5, -5, 0])
    if k % 512:
        return np.exp2(np.random.permutation(np.resize(levels, k // 32))).repeat(32)
    a = np.empty((k // 512, 16))
    for p in range(k // 512):
        a[p, :8] = np.random.permutation(np.resize(levels, 8))
        for g in range(8):
            far = levels[np.abs(levels - a[p, g]) >= 10]
            a[p, g + 8] = far[np.random.randint(len(far))]
    return np.exp2(a.ravel()).repeat(32)


def f64(x):
    return np.asarray(x).astype(np.float64)


def striped(idx):
    return np.tile(idx.reshape(-1, 16).T, (8, 1)).astype(np.uint16)


def unstriped(offs):
    return offs[:16].T.reshape(-1).astype(np.int64)


def striped8(idx):
    return np.concatenate([x.reshape(-1, 16).T for x in idx]).astype(np.uint16)


def runs(offs, k):
    lists = np.stack([offs[16 * r : 16 * r + 16].T.reshape(-1) for r in range(8)]).astype(np.int64)
    return lists[np.arange(k) % 512 // 64]


def pack_weight(w):
    k, n = w.shape
    w = f64(np.asarray(w, np.float32).astype(ml_dtypes.bfloat16)).reshape(k // 32, 32, n)
    amax = np.abs(w).max(1)
    byte = np.clip(np.where(amax > 0, np.frexp(amax)[1] - 1 + 127 - 7, 1), 1, 254)
    scaled = (w * np.exp2(127.0 - byte)[:, None, :]).reshape(k, n).astype(np.float32)
    words = np.ascontiguousarray(scaled.reshape(k // 512, 128, 4, n).transpose(0, 1, 3, 2)).astype(ml_dtypes.float8_e4m3fn).view(np.uint8)
    return words, np.ascontiguousarray(byte.astype(np.uint8).reshape(k // 512, 16, n))


def unpack_weight(words, scales):
    g, p, n, _ = words.shape
    vals = np.ascontiguousarray(words).view(ml_dtypes.float8_e4m3fn).astype(np.float64) * np.repeat(np.exp2(scales.astype(np.float64) - 127.0), 8, axis=1)[..., None]
    return vals.transpose(0, 1, 3, 2).reshape(g * 512, n)


def sigmoid(v):
    return 1.0 / (1.0 + np.exp(-np.maximum(v, -700.0)))

def planes(y):
    n, m = y.shape
    v = y.astype(np.float32).astype(ml_dtypes.bfloat16).astype(np.float64).reshape(n // 32, 32, m)
    top = np.abs(v).max(1)
    byte = np.clip(np.where(top > 0, np.frexp(top)[1] - 1 + 127 - 7, 1), 1, 254)
    codes = (v * np.exp2(127.0 - byte)[:, None, :]).reshape(n, m).astype(np.float32).astype(ml_dtypes.float8_e4m3fn).view(np.uint8)
    words = codes.reshape(n // 512, 128, 4, m).transpose(0, 1, 3, 2)
    return np.ascontiguousarray(words), np.ascontiguousarray(byte.astype(np.uint8).reshape(n // 512, 16, m))


K, T, S, H, G = 512, 1024, 512, 512, 2048


def setup_inputs():
    n = np.random.standard_normal
    s = mx_kscale(K)[:, None]
    packed_xT = pack_weight(n((K, T)) * s)
    packed_w1 = pack_weight(n((K, H)) / np.sqrt(K) / s)
    packed_w2 = pack_weight(n((K, H)) / np.sqrt(K) / s)
    packed_dT = pack_weight(n((K, G)) / s)
    return {
        "x_words": packed_xT[0],
        "x_scales": packed_xT[1],
        "w1_words": packed_w1[0],
        "w1_scales": packed_w1[1],
        "w2_words": packed_w2[0],
        "w2_scales": packed_w2[1],
        "gs": (np.random.uniform(0.5, 1.5, (K, 1)) * s).astype(np.float32),
        "d_words": packed_dT[0],
        "d_scales": packed_dT[1],
        "offs": striped(np.random.permutation(T)[:S]),
        "two": striped(np.random.permutation(T)[:S]),
        "n1": striped8(np.stack([np.random.permutation(S) for _ in range(8)])),
        "n2": striped8(np.stack([np.random.permutation(S) for _ in range(8)])),
        "k1": striped8(np.random.randint(0, G, (8, H))),
        "n3": striped8(np.stack([np.random.permutation(S) for _ in range(8)])),
        "n4": striped8(np.stack([np.random.permutation(S) for _ in range(8)])),
    }


def reference(x_words, x_scales, w1_words, w1_scales, w2_words, w2_scales, gs, d_words, d_scales, offs, two, n1, n2, k1, n3, n4):
    d_k1 = unpack_weight(d_words, d_scales)[np.arange(K)[:, None], runs(k1, K)]
    xq = unpack_weight(x_words, x_scales)[:, unstriped(offs)]
    y = unpack_weight(w1_words, w1_scales).T @ xq
    x_two = unpack_weight(x_words, x_scales)[:, unstriped(two)]
    d = unpack_weight(w2_words, w2_scales).T @ x_two
    z = f64(gs) * ((y + y[np.arange(H)[:, None], runs(n1, H)]) * (sigmoid(d + d[np.arange(H)[:, None], runs(n2, H)])))
    h = 0.0625 * ((d_k1.T @ mxq(z, 0, "e4m3")))
    pa = h[np.arange(H)[:, None], runs(n3, H)]
    pb = h[np.arange(H)[:, None], runs(n4, H)]
    mu = 0.3125 * (h + pa + pb)
    out_0 = (h - mu) / (np.sqrt((pa - mu) ** 2 + (pb - mu) ** 2 + 0.25))
    return (out_0,) + planes(out_0)

@@ -1,0 +1,245 @@
+from contextlib import ExitStack
+
+import concourse.mybir as mybir
+from concourse.masks import make_identity
+
+K, T, S, H, G = 512, 1024, 512, 512, 2048
+FLOPS = 3 * 2 * K * H * S
+
+F32 = mybir.dt.float32
+BF16 = mybir.dt.bfloat16
+I32 = mybir.dt.int32
+U32 = mybir.dt.uint32
+U16 = mybir.dt.uint16
+U8 = mybir.dt.uint8
+FP8X4 = mybir.dt.float8_e4m3fn_x4
+ALU = mybir.AluOpType
+ACT = mybir.ActivationFunctionType
+
+P = 128
+PACK = 4
+CH = 128
+PIECES = ((0, 256), (256, 384), (384, 512))
+
+M = 0.3125
+KAPPA = (1.0 - M) / 1.32
+ALPHA = -0.6
+W_SCALE = 0.0625 * KAPPA
+E_SCALE = 0.625 / KAPPA / 2.0**0.5
+D_SCALE = 1.0 / (0.6 * KAPPA) / 2.0**0.5
+
+
+def tile_picked_twqtriebstd_none_po_kernel(
+    tc, x_words, x_scales, w1_words, w1_scales, w2_words, w2_scales, gs, d_words, d_scales,
+    offs, two, n1, n2, k1, n3, n4, out_0, out_1, out_2,
+):
+    nc = tc.nc
+    with ExitStack() as ctx:
+        lists = ctx.enter_context(tc.tile_pool(name="lists", bufs=1))
+        keep = ctx.enter_context(tc.tile_pool(name="keep", bufs=1))
+        ring = ctx.enter_context(tc.tile_pool(name="ring", bufs=2))
+        psum = ctx.enter_context(tc.psum_pool(name="psum", bufs=1))
+
+        def bank(b, name):
+            return psum.tile([P, 512], F32, name=name, tag="bank%d" % b)
+
+        def words_of(dram):
+            return dram[0].rearrange("p n t -> p (n t)").bitcast(I32)
+
+        def load_list(name, dram):
+            tile = lists.tile([P, S // 16], U16, name=name)
+            nc.sync.dma_start(tile[:], dram)
+            return tile
+
+        def cols16(tile, lo, hi):
+            return tile[:, lo // 16 : hi // 16]
+
+        xw = keep.tile([P, T], I32, name="xw", align_bytes=64)
+        xs = keep.tile([P, T], U8, name="xs", align_bytes=64)
+        w1w = keep.tile([P, H], I32, name="w1w", align_bytes=64)
+        w2w = keep.tile([P, H], I32, name="w2w", align_bytes=64)
+        ws = keep.tile([P, H], U8, name="ws", tag="ws", align_bytes=64)
+        dw = keep.tile([P, G], I32, name="dw", align_bytes=64)
+        ds = keep.tile([P, G], U8, name="ds", align_bytes=64)
+        gs_sb = keep.tile([P, PACK], F32, name="gs_sb")
+        ident = keep.tile([P, P], F32, name="ident", align_bytes=64)
+        warm = keep.tile([P, 2], F32, name="warm")
+
+        nc.vector.memset(xs[:].bitcast(I32), 0)
+        nc.vector.memset(ws[:].bitcast(I32), 0)
+        nc.vector.memset(warm[:], 0.0)
+        nc.gpsimd.memset(ds[:].bitcast(I32), 0)
+        make_identity(nc, ident[:])
+
+        two_sb = load_list("two_sb", two)
+        nc.sync.dma_start(xw[:], words_of(x_words))
+        offs_sb = load_list("offs_sb", offs)
+        nc.sync.dma_start(w2w[:], words_of(w2_words))
+        for r in range(4):
+            nc.scalar.dma_start(xs[:].bitcast(I32)[r:P:32, :], x_scales[0].bitcast(I32)[r:16:4, :])
+        nc.scalar.activation(warm[:, 1:2], warm[:, 0:1], ACT.Sigmoid)
+        for r in range(4):
+            nc.sync.dma_start(ws[:].bitcast(I32)[r:P:32, :], w2_scales[0].bitcast(I32)[r:16:4, :])
+        for r in range(4):
+            nc.sync.dma_start(ws[:].bitcast(I32)[4 + r : P : 32, :], w1_scales[0].bitcast(I32)[r:16:4, :])
+        nc.sync.dma_start(w1w[:], words_of(w1_words))
+        n2_sb = load_list("n2_sb", n2)
+        nc.sync.dma_start(gs_sb[:], gs.rearrange("(p t) o -> p (t o)", t=PACK))
+        k1_sb = load_list("k1_sb", k1)
+        for e in range(2):
+            nc.sync.dma_start(ds[:].bitcast(I32)[e:P:16, :], d_scales[0].bitcast(I32)[e:16:2, :])
+        n1_sb = load_list("n1_sb", n1)
+        nc.sync.dma_start(dw[:], words_of(d_words))
+        n3_sb = load_list("n3_sb", n3)
+        n4_sb = load_list("n4_sb", n4)
+
+        def gather_words(name, table, offsets, tag):
+            picked = keep.tile([P, S], I32, name=name, tag=tag, align_bytes=64)
+            nc.vector.tensor_copy(picked[:].bitcast(U32), table[:].bitcast(U32).indirect(offsets[:]))
+            return picked
+
+        def gather_bytes(name, table, offsets, tag):
+            picked = keep.tile([P, S], U8, name=name, tag=tag, align_bytes=64)
+            nc.vector.tensor_copy(picked[:], table[:].indirect(offsets[:]))
+            return picked
+
+        def deal(name, src, dtype):
+            dealt = keep.tile([P, H], dtype, name=name, align_bytes=64)
+            nc.vector.tensor_copy(
+                dealt[:].rearrange("p (t m) -> p t m", t=PACK), src[:].rearrange("p (m t) -> p t m", t=PACK)
+            )
+            return dealt
+
+        def product(out, lhs, lhs_scale, t, rhs, rhs_scale):
+            cols = slice(t * P, (t + 1) * P)
+            nc.tensor.matmul_mx(
+                out, lhsT=lhs[:, cols].bitcast(FP8X4), lhsT_scale=lhs_scale[:, cols],
+                rhs=rhs.bitcast(FP8X4), rhs_scale=rhs_scale, start=True, stop=True,
+            )
+
+        def turn_and_add(out, sources):
+            for i, src in enumerate(sources):
+                nc.tensor.matmul(out, lhsT=src, rhs=ident[:], start=i == 0, stop=i == len(sources) - 1, is_transpose=True)
+
+        def chunk(c):
+            return slice(c * CH, (c + 1) * CH)
+
+        x2w = gather_words("x2w", xw, two_sb, "x2w")
+        x1w = gather_words("x1w", xw, offs_sb, "x1w")
+        x2s = gather_bytes("x2s", xs, two_sb, "x2s")
+        w2d = deal("w2d", w2w, I32)
+        wsd = deal("wsd", ws, U8)
+        x1s = gather_bytes("x1s", xs, offs_sb, "ws")
+        w1d = deal("w1d", w1w, I32)
+
+        d_win, y_win = [], []
+        for t in range(PACK):
+            acc = bank(t, "d_acc")
+            product(acc[:], w2d, wsd, t, x2w[:], x2s[:])
+            win = keep.tile([P, 2 * S], F32, name="d_win%d" % t, align_bytes=64)
+            nc.scalar.copy(win[:, :S], acc[:])
+            d_win.append(win)
+        for t in range(PACK):
+            acc = bank(4 + t, "y_acc")
+            product(acc[:], w1d, wsd[4:P, :], t, x1w[:], x1s[:])
+            win = keep.tile([P, S], F32, name="y_win%d" % t, tag="y_win%d" % t, align_bytes=64)
+            nc.scalar.activation(win[:], acc[:], ACT.Copy, scale=gs_sb[:, t : t + 1])
+            y_win.append(win)
+
+        gate = keep.tile([P, PACK, S], F32, name="gate", align_bytes=64)
+        for t in range(PACK):
+            picked = ring.tile([P, S], F32, name="d_picked", align_bytes=64)
+            nc.vector.tensor_copy(picked[:], d_win[t][:].indirect(n2_sb[:]))
+            u = bank(t, "u")
+            for c in range(4):
+                turn_and_add(u[:, chunk(c)], [d_win[t][:, chunk(c)], picked[:, chunk(c)]])
+            nc.scalar.activation(gate[:, t, :], u[:], ACT.Sigmoid)
+        nc.scalar.activation(warm[:, 1:2], gate[:, PACK - 1, 0:1], ACT.Abs_reciprocal_sqrt)
+
+        dks = gather_bytes("dks", ds, k1_sb, "dks")
+        dsd = deal("dsd", dks, U8)
+        for e in range(2):
+            nc.sync.dma_start(dsd[:].bitcast(I32)[2 + e : P : 32, :], dsd[:].bitcast(I32)[16 + e : P : 32, :])
+
+        v = [bank(4 + c, "v") for c in range(4)]
+        for lo, hi in PIECES:
+            for t in range(PACK):
+                picked = ring.tile([P, hi - lo], F32, name="y_picked", align_bytes=64, bufs=4)
+                nc.vector.tensor_copy(picked[:], y_win[t][:].indirect(cols16(n1_sb, lo, hi)))
+                for c in range(lo // CH, hi // CH):
+                    turn_and_add(v[c][:, chunk(t)], [y_win[t][:, chunk(c)], picked[:, chunk(c - lo // CH)]])
+
+        dkw = gather_words("dkw", dw, k1_sb, "y_win2")
+        dwd = deal("dwd", dkw, I32)
+
+        z_codes = keep.tile([P, S], I32, name="z_codes", align_bytes=64)
+        z_scales = keep.tile([P, S], U8, name="z_scales", align_bytes=64)
+        h_acc = [bank(t, "h_acc") for t in range(PACK)]
+        w_win = [keep.tile([P, 2 * S if t < PACK - 1 else S], F32, name="w_win%d" % t, align_bytes=64) for t in range(PACK)]
+        for lo, hi in PIECES:
+            z_in = keep.tile([P, (hi - lo) * PACK], BF16, name="z_in%d" % lo, align_bytes=64)
+            for c in range(lo // CH, hi // CH):
+                z_turned = ring.tile([P, 2, P, 2], BF16, name="z_turned", align_bytes=64)
+                nc.vector.tensor_tensor(
+                    z_turned[:],
+                    v[c][:].rearrange("j (u e p) -> j u p e", u=2, e=2),
+                    gate[:, :, chunk(c)].rearrange("j (u e) p -> j u p e", u=2),
+                    ALU.mult,
+                )
+                back = bank(4 + c, "back")
+                z_pairs = z_turned[:].rearrange("j u p e -> j (u p e)").bitcast(F32)
+                for u in range(2):
+                    nc.tensor.transpose(back[:, chunk(u)], z_pairs[:, chunk(u)], ident[:])
+                first = (c - lo // CH) * 2 * CH
+                nc.scalar.copy(
+                    z_in[:].bitcast(F32)[:, first : first + 2 * CH].rearrange("p (j u) -> p j u", u=2),
+                    back[:, : 2 * CH].rearrange("p (u j) -> p j u", u=2),
+                )
+            nc.vector.quantize_mx(z_codes[:, lo:hi].bitcast(FP8X4), z_scales[:, lo:hi], z_in[:])
+            for t in range(PACK):
+                product(h_acc[t][:, lo:hi], dwd, dsd, t, z_codes[:, lo:hi], z_scales[:, lo:hi])
+                if hi % 256 == 0:
+                    nc.scalar.activation(w_win[t][:, hi - 256 : hi], h_acc[t][:, hi - 256 : hi], ACT.Copy, scale=W_SCALE)
+
+        result = keep.tile([P, PACK, S], F32, name="result", align_bytes=64)
+        o_codes = keep.tile([P, S], I32, name="o_codes", align_bytes=64)
+        o_scales = keep.tile([P, S], U8, name="o_scales", align_bytes=64)
+        out_rows = out_0.rearrange("(p t) j -> p t j", t=PACK)
+        units = [(t, 0, S) for t in range(PACK - 1)] + [(PACK - 1, lo, hi) for lo, hi in PIECES]
+        for i, (t, lo, hi) in enumerate(units):
+            n = hi - lo
+            w = w_win[t]
+            a = ring.tile([P, n], F32, name="a", align_bytes=64)
+            b = ring.tile([P, n], F32, name="b", align_bytes=64)
+            both = ring.tile([P, n], F32, name="both", align_bytes=64)
+            num = ring.tile([P, n], F32, name="num", align_bytes=64, bufs=3)
+            nc.vector.tensor_scalar(a[:], w[:].indirect(cols16(n3_sb, lo, hi)), ALPHA, 0.0, ALU.mult, ALU.add)
+            nc.vector.tensor_scalar(b[:], w[:].indirect(cols16(n4_sb, lo, hi)), -ALPHA, 0.0, ALU.mult, ALU.add)
+            nc.vector.tensor_tensor(both[:], a[:], b[:], ALU.subtract)
+            nc.vector.scalar_tensor_tensor(num[:], w[:, lo:hi], 1.32, both[:], ALU.mult, ALU.add)
+            diff = bank((4 + 3 * i) % 8, "diff")
+            even = bank((5 + 3 * i) % 8, "even")
+            total = bank((6 + 3 * i) % 8, "total")
+            diff2 = ring.tile([P, n], F32, name="diff2", align_bytes=64)
+            even2 = ring.tile([P, n], F32, name="even2", align_bytes=64)
+            root = ring.tile([P, n], F32, name="root", align_bytes=64)
+            for c in range(n // CH):
+                turn_and_add(diff[:, chunk(c)], [a[:, chunk(c)], b[:, chunk(c)]])
+            nc.scalar.activation(diff2[:], diff[:, :n], ACT.Square, scale=D_SCALE)
+            for c in range(n // CH):
+                turn_and_add(even[:, chunk(c)], [w[:, lo + c * CH : lo + (c + 1) * CH], both[:, chunk(c)]])
+            nc.scalar.activation(even2[:], even[:, :n], ACT.Square, scale=E_SCALE)
+            for c in range(n // CH):
+                turn_and_add(total[:, chunk(c)], [diff2[:, chunk(c)], even2[:, chunk(c)]])
+            nc.scalar.activation(root[:], total[:, :n], ACT.Abs_reciprocal_sqrt, bias=0.25)
+            nc.vector.tensor_tensor(result[:, t, lo:hi], num[:], root[:], ALU.mult)
+            nc.sync.dma_start(out_rows[:, t, lo:hi], result[:, t, lo:hi])
+            if t == PACK - 1:
+                o_in = ring.tile([P, n, PACK], BF16, name="o_in", align_bytes=64, bufs=3)
+                nc.vector.tensor_copy(o_in[:], result[:, :, lo:hi].rearrange("p t j -> p j t"))
+                nc.vector.quantize_mx(
+                    o_codes[:, lo:hi].bitcast(FP8X4), o_scales[:, lo:hi], o_in[:].rearrange("p j t -> p (j t)")
+                )
+                nc.sync.dma_start(words_of(out_1)[:, lo:hi], o_codes[:, lo:hi])
+        for q in range(4):
+            (nc.scalar if q % 2 else nc.sync).dma_start(out_2[0].bitcast(I32)[4 * q : 4 * q + 4, :], o_scales[:].bitcast(I32)[32 * q : 32 * q + 4, :])

@@ -21,12 +21,27 @@ PACK = 4
 CH = 128
 PIECES = ((0, 256), (256, 384), (384, 512))
 
+WPACK = True
+GDEAL = False
+GOPS = ()
+GLAST = {"both":3,"diff":3,"out":2}
+BA = 2
+BB = 2
+BBOTH = 2
+BSQ = 2
+DESIGN = (20,20,20,20,0,0)
+SCAST = (0,)
+UNITS = [(0,0,512),(1,0,512),(2,0,512),(3,0,256),(3,256,384),(3,384,512)]
+BANKS = [(5+i)%8 for i in range(40)]
+DKW_AT = 3
+DKW_TAG = "dkw"
+ZPIECES = ((0,256),(256,384),(384,512))
+WCOPY = {(384,0):0,(512,0):384,(512,1):0,(512,2):0,(512,3):0}
 M = 0.3125
-KAPPA = (1.0 - M) / 1.32
-ALPHA = -0.6
+KAPPA = -M
 W_SCALE = 0.0625 * KAPPA
-E_SCALE = 0.625 / KAPPA / 2.0**0.5
-D_SCALE = 1.0 / (0.6 * KAPPA) / 2.0**0.5
+E_SCALE = (1.0 - 2.0 * M) / M / 2.0**0.5
+D_SCALE = 1.0 / M / 2.0**0.5
 
 
 def tile_picked_twqtriebstd_none_po_kernel(
@@ -58,36 +73,43 @@ def tile_picked_twqtriebstd_none_po_kernel(
         xs = keep.tile([P, T], U8, name="xs", align_bytes=64)
         w1w = keep.tile([P, H], I32, name="w1w", align_bytes=64)
         w2w = keep.tile([P, H], I32, name="w2w", align_bytes=64)
-        ws = keep.tile([P, H], U8, name="ws", tag="ws", align_bytes=64)
+        w1s = keep.tile([P, H], U8, name="w1s", align_bytes=64)
+        w2s = keep.tile([P, H], U8, name="w2s", tag="w2s", align_bytes=64)
+        ws = w2s if WPACK else None
         dw = keep.tile([P, G], I32, name="dw", align_bytes=64)
         ds = keep.tile([P, G], U8, name="ds", align_bytes=64)
         gs_sb = keep.tile([P, PACK], F32, name="gs_sb")
         ident = keep.tile([P, P], F32, name="ident", align_bytes=64)
         warm = keep.tile([P, 2], F32, name="warm")
 
-        nc.vector.memset(xs[:].bitcast(I32), 0)
-        nc.vector.memset(ws[:].bitcast(I32), 0)
+        nc.gpsimd.memset(xs[:].bitcast(I32), 0)
+        nc.gpsimd.memset(w2s[:].bitcast(I32), 0)
+        if not WPACK:
+            nc.gpsimd.memset(w1s[:].bitcast(I32), 0)
+        nc.vector.memset(ds[:].bitcast(I32), 0)
         nc.vector.memset(warm[:], 0.0)
-        nc.gpsimd.memset(ds[:].bitcast(I32), 0)
         make_identity(nc, ident[:])
 
         two_sb = load_list("two_sb", two)
         nc.sync.dma_start(xw[:], words_of(x_words))
         offs_sb = load_list("offs_sb", offs)
-        nc.sync.dma_start(w2w[:], words_of(w2_words))
         for r in range(4):
             nc.scalar.dma_start(xs[:].bitcast(I32)[r:P:32, :], x_scales[0].bitcast(I32)[r:16:4, :])
         nc.scalar.activation(warm[:, 1:2], warm[:, 0:1], ACT.Sigmoid)
+        nc.sync.dma_start(w2w[:], words_of(w2_words))
         for r in range(4):
-            nc.sync.dma_start(ws[:].bitcast(I32)[r:P:32, :], w2_scales[0].bitcast(I32)[r:16:4, :])
+            nc.sync.dma_start(w2s[:].bitcast(I32)[r:P:32, :], w2_scales[0].bitcast(I32)[r:16:4, :])
+        if not WPACK:
+            nc.sync.dma_start(w1w[:], words_of(w1_words))
         for r in range(4):
-            nc.sync.dma_start(ws[:].bitcast(I32)[4 + r : P : 32, :], w1_scales[0].bitcast(I32)[r:16:4, :])
-        nc.sync.dma_start(w1w[:], words_of(w1_words))
-        n2_sb = load_list("n2_sb", n2)
-        nc.sync.dma_start(gs_sb[:], gs.rearrange("(p t) o -> p (t o)", t=PACK))
+            nc.sync.dma_start((w2s[:].bitcast(I32)[4 + r : P : 32, :] if WPACK else w1s[:].bitcast(I32)[r:P:32, :]), w1_scales[0].bitcast(I32)[r:16:4, :])
+        if WPACK:
+            nc.sync.dma_start(w1w[:], words_of(w1_words))
         k1_sb = load_list("k1_sb", k1)
         for e in range(2):
             nc.sync.dma_start(ds[:].bitcast(I32)[e:P:16, :], d_scales[0].bitcast(I32)[e:16:2, :])
+        n2_sb = load_list("n2_sb", n2)
+        nc.sync.dma_start(gs_sb[:], gs.rearrange("(p t) o -> p (t o)", t=PACK))
         n1_sb = load_list("n1_sb", n1)
         nc.sync.dma_start(dw[:], words_of(d_words))
         n3_sb = load_list("n3_sb", n3)
@@ -103,9 +125,9 @@ def tile_picked_twqtriebstd_none_po_kernel(
             nc.vector.tensor_copy(picked[:], table[:].indirect(offsets[:]))
             return picked
 
-        def deal(name, src, dtype):
+        def deal(engine, name, src, dtype):
             dealt = keep.tile([P, H], dtype, name=name, align_bytes=64)
-            nc.vector.tensor_copy(
+            engine.tensor_copy(
                 dealt[:].rearrange("p (t m) -> p t m", t=PACK), src[:].rearrange("p (m t) -> p t m", t=PACK)
             )
             return dealt
@@ -124,121 +146,137 @@ def tile_picked_twqtriebstd_none_po_kernel(
         def chunk(c):
             return slice(c * CH, (c + 1) * CH)
 
+        dealer = nc.gpsimd if GDEAL else nc.vector
         x2w = gather_words("x2w", xw, two_sb, "x2w")
         x1w = gather_words("x1w", xw, offs_sb, "x1w")
         x2s = gather_bytes("x2s", xs, two_sb, "x2s")
-        w2d = deal("w2d", w2w, I32)
-        wsd = deal("wsd", ws, U8)
-        x1s = gather_bytes("x1s", xs, offs_sb, "ws")
-        w1d = deal("w1d", w1w, I32)
+        w2d = deal(dealer, "w2d", w2w, I32)
+        w2sd = deal(dealer, "w2sd", w2s, U8)
+        x1s = gather_bytes("x1s", xs, offs_sb, "x1s" if GDEAL else "w2s")
+        w1d = deal(dealer, "w1d", w1w, I32)
+        w1sd = w2sd[4:P, :] if WPACK else deal(dealer, "w1sd", w1s, U8)
 
-        d_win, y_win = [], []
-        for t in range(PACK):
-            acc = bank(t, "d_acc")
-            product(acc[:], w2d, wsd, t, x2w[:], x2s[:])
-            win = keep.tile([P, 2 * S], F32, name="d_win%d" % t, align_bytes=64)
-            nc.scalar.copy(win[:, :S], acc[:])
-            d_win.append(win)
-        for t in range(PACK):
-            acc = bank(4 + t, "y_acc")
-            product(acc[:], w1d, wsd[4:P, :], t, x1w[:], x1s[:])
-            win = keep.tile([P, S], F32, name="y_win%d" % t, tag="y_win%d" % t, align_bytes=64)
-            nc.scalar.activation(win[:], acc[:], ACT.Copy, scale=gs_sb[:, t : t + 1])
-            y_win.append(win)
+        def windows(name, banks, lhs, lhs_scale, rhs, rhs_scale, scale):
+            pairs = []
+            for t in range(PACK):
+                acc = bank(banks + t, name + "_acc")
+                product(acc[:], lhs, lhs_scale, t, rhs[:], rhs_scale[:])
+                win = keep.tile([P, 2 * S], F32, name="%s_win%d" % (name, t), tag="%s_win%d" % (name, t), align_bytes=64)
+                plain = keep.tile([P, S], F32, name="%s_plain%d" % (name, t), tag="%s_plain%d" % (name, t), align_bytes=64)
+                for copy in (win[:, :S], plain[:]):
+                    nc.scalar.activation(copy, acc[:], ACT.Copy, scale=scale(t))
+                pairs.append((win, plain))
+            return pairs
 
-        gate = keep.tile([P, PACK, S], F32, name="gate", align_bytes=64)
-        for t in range(PACK):
-            picked = ring.tile([P, S], F32, name="d_picked", align_bytes=64)
-            nc.vector.tensor_copy(picked[:], d_win[t][:].indirect(n2_sb[:]))
-            u = bank(t, "u")
-            for c in range(4):
-                turn_and_add(u[:, chunk(c)], [d_win[t][:, chunk(c)], picked[:, chunk(c)]])
-            nc.scalar.activation(gate[:, t, :], u[:], ACT.Sigmoid)
-        nc.scalar.activation(warm[:, 1:2], gate[:, PACK - 1, 0:1], ACT.Abs_reciprocal_sqrt)
+        d_pairs = windows("d", 0, w2d, w2sd, x2w, x2s, lambda t: 1.0)
+        y_pairs = windows("y", 4, w1d, w1sd, x1w, x1s, lambda t: gs_sb[:, t : t + 1])
 
         dks = gather_bytes("dks", ds, k1_sb, "dks")
-        dsd = deal("dsd", dks, U8)
+        dsd = deal(nc.vector, "dsd", dks, U8)
         for e in range(2):
             nc.sync.dma_start(dsd[:].bitcast(I32)[2 + e : P : 32, :], dsd[:].bitcast(I32)[16 + e : P : 32, :])
 
-        v = [bank(4 + c, "v") for c in range(4)]
-        for lo, hi in PIECES:
-            for t in range(PACK):
-                picked = ring.tile([P, hi - lo], F32, name="y_picked", align_bytes=64, bufs=4)
-                nc.vector.tensor_copy(picked[:], y_win[t][:].indirect(cols16(n1_sb, lo, hi)))
-                for c in range(lo // CH, hi // CH):
-                    turn_and_add(v[c][:, chunk(t)], [y_win[t][:, chunk(c)], picked[:, chunk(c - lo // CH)]])
+        gate = keep.tile([P, PACK, S], F32, name="gate", align_bytes=64)
+        for t, (win, plain) in enumerate(d_pairs):
+            u = ring.tile([P, S], F32, name="u", align_bytes=64, bufs=4)
+            nc.vector.tensor_tensor(u[:], win[:].indirect(n2_sb[:]), plain[:], ALU.add)
+            nc.scalar.activation(gate[:, t, :], u[:], ACT.Sigmoid)
+        nc.scalar.activation(warm[:, 1:2], gate[:, PACK - 1, 0:1], ACT.Abs_reciprocal_sqrt)
+        v = keep.tile([P, PACK, S], F32, name="v", align_bytes=64)
+        for t, (win, plain) in enumerate(y_pairs):
+            nc.vector.tensor_tensor(v[:, t, :], win[:].indirect(n1_sb[:]), plain[:], ALU.add)
+            if t == DKW_AT:
+                dkw = gather_words("dkw", dw, k1_sb, DKW_TAG)
+                dwd = deal(nc.vector, "dwd", dkw, I32)
 
-        dkw = gather_words("dkw", dw, k1_sb, "y_win2")
-        dwd = deal("dwd", dkw, I32)
+        def by_pairs(rows):
+            return rows.rearrange("p t (c i) -> p c t i", i=2)
+
+        def woven(tile):
+            return tile[:].rearrange("p (c i t) -> p c t i", i=2, t=PACK)
 
         z_codes = keep.tile([P, S], I32, name="z_codes", align_bytes=64)
         z_scales = keep.tile([P, S], U8, name="z_scales", align_bytes=64)
         h_acc = [bank(t, "h_acc") for t in range(PACK)]
-        w_win = [keep.tile([P, 2 * S if t < PACK - 1 else S], F32, name="w_win%d" % t, align_bytes=64) for t in range(PACK)]
-        for lo, hi in PIECES:
+        w_win = [keep.tile([P, 2 * S if (t, 0, S) in UNITS else S], F32, name="w_win%d" % t, align_bytes=64) for t in range(PACK)]
+        for lo, hi in ZPIECES:
             z_in = keep.tile([P, (hi - lo) * PACK], BF16, name="z_in%d" % lo, align_bytes=64)
-            for c in range(lo // CH, hi // CH):
-                z_turned = ring.tile([P, 2, P, 2], BF16, name="z_turned", align_bytes=64)
-                nc.vector.tensor_tensor(
-                    z_turned[:],
-                    v[c][:].rearrange("j (u e p) -> j u p e", u=2, e=2),
-                    gate[:, :, chunk(c)].rearrange("j (u e) p -> j u p e", u=2),
-                    ALU.mult,
-                )
-                back = bank(4 + c, "back")
-                z_pairs = z_turned[:].rearrange("j u p e -> j (u p e)").bitcast(F32)
-                for u in range(2):
-                    nc.tensor.transpose(back[:, chunk(u)], z_pairs[:, chunk(u)], ident[:])
-                first = (c - lo // CH) * 2 * CH
-                nc.scalar.copy(
-                    z_in[:].bitcast(F32)[:, first : first + 2 * CH].rearrange("p (j u) -> p j u", u=2),
-                    back[:, : 2 * CH].rearrange("p (u j) -> p j u", u=2),
-                )
+            nc.vector.tensor_tensor(woven(z_in), by_pairs(v[:, :, lo:hi]), by_pairs(gate[:, :, lo:hi]), ALU.mult)
             nc.vector.quantize_mx(z_codes[:, lo:hi].bitcast(FP8X4), z_scales[:, lo:hi], z_in[:])
             for t in range(PACK):
-                product(h_acc[t][:, lo:hi], dwd, dsd, t, z_codes[:, lo:hi], z_scales[:, lo:hi])
-                if hi % 256 == 0:
-                    nc.scalar.activation(w_win[t][:, hi - 256 : hi], h_acc[t][:, hi - 256 : hi], ACT.Copy, scale=W_SCALE)
+                acc = bank(4, "h_last") if (hi, t) == (S, 0) else h_acc[t]
+                product(acc[:, lo:hi], dwd, dsd, t, z_codes[:, lo:hi], z_scales[:, lo:hi])
+                if (hi, t) in WCOPY:
+                    nc.scalar.activation(w_win[t][:, WCOPY[hi, t] : hi], acc[:, WCOPY[hi, t] : hi], ACT.Copy, scale=W_SCALE)
 
         result = keep.tile([P, PACK, S], F32, name="result", align_bytes=64)
         o_codes = keep.tile([P, S], I32, name="o_codes", align_bytes=64)
         o_scales = keep.tile([P, S], U8, name="o_scales", align_bytes=64)
         out_rows = out_0.rearrange("(p t) j -> p t j", t=PACK)
-        units = [(t, 0, S) for t in range(PACK - 1)] + [(PACK - 1, lo, hi) for lo, hi in PIECES]
+        units = UNITS
+        w_even = {}
         for i, (t, lo, hi) in enumerate(units):
             n = hi - lo
             w = w_win[t]
-            a = ring.tile([P, n], F32, name="a", align_bytes=64)
-            b = ring.tile([P, n], F32, name="b", align_bytes=64)
-            both = ring.tile([P, n], F32, name="both", align_bytes=64)
+            design = DESIGN[i]
+            eng = {k: nc.gpsimd if k in GOPS and t < GLAST[k] else nc.vector for k in ("both", "diff", "out")}
+            a = ring.tile([P, n], F32, name="a", align_bytes=64, bufs=BA)
+            both = ring.tile([P, n], F32, name="both", align_bytes=64, bufs=BBOTH)
             num = ring.tile([P, n], F32, name="num", align_bytes=64, bufs=3)
-            nc.vector.tensor_scalar(a[:], w[:].indirect(cols16(n3_sb, lo, hi)), ALPHA, 0.0, ALU.mult, ALU.add)
-            nc.vector.tensor_scalar(b[:], w[:].indirect(cols16(n4_sb, lo, hi)), -ALPHA, 0.0, ALU.mult, ALU.add)
-            nc.vector.tensor_tensor(both[:], a[:], b[:], ALU.subtract)
-            nc.vector.scalar_tensor_tensor(num[:], w[:, lo:hi], 1.32, both[:], ALU.mult, ALU.add)
-            diff = bank((4 + 3 * i) % 8, "diff")
-            even = bank((5 + 3 * i) % 8, "even")
-            total = bank((6 + 3 * i) % 8, "total")
-            diff2 = ring.tile([P, n], F32, name="diff2", align_bytes=64)
-            even2 = ring.tile([P, n], F32, name="even2", align_bytes=64)
+            dif = ring.tile([P, n], F32, name="dif", align_bytes=64)
+            diff2 = ring.tile([P, n], F32, name="diff2", align_bytes=64, bufs=BSQ)
+            even2 = ring.tile([P, n], F32, name="even2", align_bytes=64, bufs=BSQ)
             root = ring.tile([P, n], F32, name="root", align_bytes=64)
-            for c in range(n // CH):
-                turn_and_add(diff[:, chunk(c)], [a[:, chunk(c)], b[:, chunk(c)]])
-            nc.scalar.activation(diff2[:], diff[:, :n], ACT.Square, scale=D_SCALE)
-            for c in range(n // CH):
-                turn_and_add(even[:, chunk(c)], [w[:, lo + c * CH : lo + (c + 1) * CH], both[:, chunk(c)]])
-            nc.scalar.activation(even2[:], even[:, :n], ACT.Square, scale=E_SCALE)
-            for c in range(n // CH):
-                turn_and_add(total[:, chunk(c)], [diff2[:, chunk(c)], even2[:, chunk(c)]])
-            nc.scalar.activation(root[:], total[:, :n], ACT.Abs_reciprocal_sqrt, bias=0.25)
-            nc.vector.tensor_tensor(result[:, t, lo:hi], num[:], root[:], ALU.mult)
+            nc.vector.tensor_scalar(a[:], w[:].indirect(cols16(n3_sb, lo, hi)), -1.0, 0.0, ALU.mult, ALU.add)
+            nc.vector.tensor_tensor(both[:], w[:].indirect(cols16(n4_sb, lo, hi)), a[:], ALU.subtract)
+            if design <= 20:
+                nc.vector.scalar_tensor_tensor(dif[:], a[:], 2.0, both[:], ALU.mult, ALU.add)
+            if design <= 12:
+                ev = ring.tile([P, n], F32, name="ev", align_bytes=64)
+                nc.vector.scalar_tensor_tensor(ev[:], w[:, lo:hi], -5.0 / 3.0, both[:], ALU.mult, ALU.add)
+            nc.vector.scalar_tensor_tensor(num[:], w[:, lo:hi], -2.2, both[:], ALU.mult, ALU.add)
+            if design >= 20:
+                we = ring.tile([P, n], F32, name="we", align_bytes=64)
+                nc.scalar.activation(we[:], w[:, lo:hi], ACT.Copy, scale=-5.0 / 3.0)
+                diff = bank(BANKS[3 * i], "diff")
+                even = bank(BANKS[3 * i + 1], "even")
+                total = bank(BANKS[3 * i + 2], "total")
+                for c in range(n // CH):
+                    turn_and_add(even[:, chunk(c)], [both[:, chunk(c)], we[:, chunk(c)]])
+                nc.scalar.activation(even2[:], even[:, :n], ACT.Square, scale=E_SCALE)
+                for c in range(n // CH):
+                    turn_and_add(diff[:, chunk(c)], [dif[:, chunk(c)]] if design == 20 else [both[:, chunk(c)], a[:, chunk(c)], a[:, chunk(c)]])
+                nc.scalar.activation(diff2[:], diff[:, :n], ACT.Square, scale=D_SCALE)
+                for c in range(n // CH):
+                    turn_and_add(total[:, chunk(c)], [diff2[:, chunk(c)], even2[:, chunk(c)]])
+                nc.scalar.activation(root[:], total[:, :n], ACT.Abs_reciprocal_sqrt, bias=0.25)
+                eng["out"].tensor_tensor(result[:, t, lo:hi], num[:], root[:], ALU.mult)
+            else:
+                nc.scalar.activation(diff2[:], dif[:], ACT.Square, scale=D_SCALE)
+                nc.scalar.activation(even2[:], ev[:], ACT.Square, scale=E_SCALE)
+                if design == 12:
+                    total = bank(BANKS[3 * i], "total")
+                    rback = bank(BANKS[3 * i + 1], "rback")
+                    for c in range(n // CH):
+                        turn_and_add(total[:, chunk(c)], [even2[:, chunk(c)], diff2[:, chunk(c)]])
+                    nc.scalar.activation(root[:], total[:, :n], ACT.Abs_reciprocal_sqrt, bias=0.25)
+                    for c in range(n // CH):
+                        turn_and_add(rback[:, chunk(c)], [root[:, chunk(c)]])
+                    nc.vector.tensor_tensor(result[:, t, lo:hi], rback[:, :n], num[:], ALU.mult)
+                else:
+                    tot = ring.tile([P, n], F32, name="tot", align_bytes=64)
+                    nc.vector.tensor_tensor(tot[:], even2[:], diff2[:], ALU.add)
+                    nc.scalar.activation(root[:], tot[:], ACT.Abs_reciprocal_sqrt, bias=0.25)
+                    nc.vector.tensor_tensor(result[:, t, lo:hi], num[:], root[:], ALU.mult)
             nc.sync.dma_start(out_rows[:, t, lo:hi], result[:, t, lo:hi])
             if t == PACK - 1:
-                o_in = ring.tile([P, n, PACK], BF16, name="o_in", align_bytes=64, bufs=3)
-                nc.vector.tensor_copy(o_in[:], result[:, :, lo:hi].rearrange("p t j -> p j t"))
+                o_in = ring.tile([P, n * PACK], BF16, name="o_in", align_bytes=64, bufs=3)
+                if lo in SCAST:
+                    nc.scalar.copy(woven(o_in), by_pairs(result[:, :, lo:hi]))
+                else:
+                    nc.vector.tensor_copy(woven(o_in), by_pairs(result[:, :, lo:hi]))
                 nc.vector.quantize_mx(
-                    o_codes[:, lo:hi].bitcast(FP8X4), o_scales[:, lo:hi], o_in[:].rearrange("p j t -> p (j t)")
+                    o_codes[:, lo:hi].bitcast(FP8X4), o_scales[:, lo:hi], o_in[:]
                 )
                 nc.sync.dma_start(words_of(out_1)[:, lo:hi], o_codes[:, lo:hi])
         for q in range(4):

@@ -21,22 +21,26 @@ PACK = 4
 CH = 128
 PIECES = ((0, 256), (256, 384), (384, 512))
 
-WPACK = True
-GDEAL = False
+WPACK = False
+GDEAL = True
 GOPS = ()
 GLAST = {"both":3,"diff":3,"out":2}
 BA = 2
 BB = 2
 BBOTH = 2
-BSQ = 2
-DESIGN = (20,20,20,20,0,0)
+BSQ = 3
+DESIGN = (20,20,20,20,20,20,20,20,0)
 SCAST = (0,)
-UNITS = [(0,0,512),(1,0,512),(2,0,512),(3,0,256),(3,256,384),(3,384,512)]
-BANKS = [(5+i)%8 for i in range(40)]
+UNITS = [(0,0,256),(1,0,256),(2,0,256),(3,0,256),(0,256,512),(1,256,512),(2,256,512),(3,256,384),(3,384,512)]
+BANKS = [(5+i)%7 for i in range(40)]
 DKW_AT = 3
 DKW_TAG = "dkw"
 ZPIECES = ((0,256),(256,384),(384,512))
-WCOPY = {(384,0):0,(512,0):384,(512,1):0,(512,2):0,(512,3):0}
+WCOPY = {384:0,512:384}
+X1TAG = "x1w"
+FILL = (0,)*9
+FILL0 = 0
+FILL0_T = 1
 M = 0.3125
 KAPPA = -M
 W_SCALE = 0.0625 * KAPPA
@@ -72,7 +76,7 @@ def tile_picked_twqtriebstd_none_po_kernel(
         xw = keep.tile([P, T], I32, name="xw", align_bytes=64)
         xs = keep.tile([P, T], U8, name="xs", align_bytes=64)
         w1w = keep.tile([P, H], I32, name="w1w", align_bytes=64)
-        w2w = keep.tile([P, H], I32, name="w2w", align_bytes=64)
+        w2w = keep.tile([P, H], I32, name="w2w", tag="w2w", align_bytes=64)
         w1s = keep.tile([P, H], U8, name="w1s", align_bytes=64)
         w2s = keep.tile([P, H], U8, name="w2s", tag="w2s", align_bytes=64)
         ws = w2s if WPACK else None
@@ -82,29 +86,26 @@ def tile_picked_twqtriebstd_none_po_kernel(
         ident = keep.tile([P, P], F32, name="ident", align_bytes=64)
         warm = keep.tile([P, 2], F32, name="warm")
 
-        nc.gpsimd.memset(xs[:].bitcast(I32), 0)
-        nc.gpsimd.memset(w2s[:].bitcast(I32), 0)
-        if not WPACK:
-            nc.gpsimd.memset(w1s[:].bitcast(I32), 0)
+        def load_scales(tile, dram):
+            rows = dram[0].bitcast(I32)
+            for r in range(4):
+                nc.sync.dma_start(
+                    tile[:].bitcast(I32)[r:P:4, :], rows[r:16:4, :].unsqueeze(1).broadcast_to([4, 8, rows.shape[1]])
+                )
+
         nc.vector.memset(ds[:].bitcast(I32), 0)
         nc.vector.memset(warm[:], 0.0)
         make_identity(nc, ident[:])
 
         two_sb = load_list("two_sb", two)
-        nc.sync.dma_start(xw[:], words_of(x_words))
+        load_scales(xs, x_scales)
         offs_sb = load_list("offs_sb", offs)
-        for r in range(4):
-            nc.scalar.dma_start(xs[:].bitcast(I32)[r:P:32, :], x_scales[0].bitcast(I32)[r:16:4, :])
+        nc.sync.dma_start(xw[:], words_of(x_words))
         nc.scalar.activation(warm[:, 1:2], warm[:, 0:1], ACT.Sigmoid)
         nc.sync.dma_start(w2w[:], words_of(w2_words))
-        for r in range(4):
-            nc.sync.dma_start(w2s[:].bitcast(I32)[r:P:32, :], w2_scales[0].bitcast(I32)[r:16:4, :])
-        if not WPACK:
-            nc.sync.dma_start(w1w[:], words_of(w1_words))
-        for r in range(4):
-            nc.sync.dma_start((w2s[:].bitcast(I32)[4 + r : P : 32, :] if WPACK else w1s[:].bitcast(I32)[r:P:32, :]), w1_scales[0].bitcast(I32)[r:16:4, :])
-        if WPACK:
-            nc.sync.dma_start(w1w[:], words_of(w1_words))
+        load_scales(w2s, w2_scales)
+        nc.sync.dma_start(w1w[:], words_of(w1_words))
+        load_scales(w1s, w1_scales)
         k1_sb = load_list("k1_sb", k1)
         for e in range(2):
             nc.sync.dma_start(ds[:].bitcast(I32)[e:P:16, :], d_scales[0].bitcast(I32)[e:16:2, :])
@@ -125,8 +126,8 @@ def tile_picked_twqtriebstd_none_po_kernel(
             nc.vector.tensor_copy(picked[:], table[:].indirect(offsets[:]))
             return picked
 
-        def deal(engine, name, src, dtype):
-            dealt = keep.tile([P, H], dtype, name=name, align_bytes=64)
+        def deal(engine, name, src, dtype, tag=""):
+            dealt = keep.tile([P, H], dtype, name=name, tag=tag or name, align_bytes=64)
             engine.tensor_copy(
                 dealt[:].rearrange("p (t m) -> p t m", t=PACK), src[:].rearrange("p (m t) -> p t m", t=PACK)
             )
@@ -147,13 +148,17 @@ def tile_picked_twqtriebstd_none_po_kernel(
             return slice(c * CH, (c + 1) * CH)
 
         dealer = nc.gpsimd if GDEAL else nc.vector
-        x2w = gather_words("x2w", xw, two_sb, "x2w")
-        x1w = gather_words("x1w", xw, offs_sb, "x1w")
         x2s = gather_bytes("x2s", xs, two_sb, "x2s")
+        x1s = gather_bytes("x1s", xs, offs_sb, "x1s")
+        x2w = gather_words("x2w", xw, two_sb, "x2w")
         w2d = deal(dealer, "w2d", w2w, I32)
         w2sd = deal(dealer, "w2sd", w2s, U8)
-        x1s = gather_bytes("x1s", xs, offs_sb, "x1s" if GDEAL else "w2s")
+        x1w = gather_words("x1w", xw, offs_sb, X1TAG)
+        dks = gather_bytes("dks", ds, k1_sb, "dks")
         w1d = deal(dealer, "w1d", w1w, I32)
+        dsd = deal(nc.vector, "dsd", dks, U8)
+        for e in range(2):
+            nc.sync.dma_start(dsd[:].bitcast(I32)[2 + e : P : 32, :], dsd[:].bitcast(I32)[16 + e : P : 32, :])
         w1sd = w2sd[4:P, :] if WPACK else deal(dealer, "w1sd", w1s, U8)
 
         def windows(name, banks, lhs, lhs_scale, rhs, rhs_scale, scale):
@@ -171,11 +176,6 @@ def tile_picked_twqtriebstd_none_po_kernel(
         d_pairs = windows("d", 0, w2d, w2sd, x2w, x2s, lambda t: 1.0)
         y_pairs = windows("y", 4, w1d, w1sd, x1w, x1s, lambda t: gs_sb[:, t : t + 1])
 
-        dks = gather_bytes("dks", ds, k1_sb, "dks")
-        dsd = deal(nc.vector, "dsd", dks, U8)
-        for e in range(2):
-            nc.sync.dma_start(dsd[:].bitcast(I32)[2 + e : P : 32, :], dsd[:].bitcast(I32)[16 + e : P : 32, :])
-
         gate = keep.tile([P, PACK, S], F32, name="gate", align_bytes=64)
         for t, (win, plain) in enumerate(d_pairs):
             u = ring.tile([P, S], F32, name="u", align_bytes=64, bufs=4)
@@ -187,7 +187,7 @@ def tile_picked_twqtriebstd_none_po_kernel(
             nc.vector.tensor_tensor(v[:, t, :], win[:].indirect(n1_sb[:]), plain[:], ALU.add)
             if t == DKW_AT:
                 dkw = gather_words("dkw", dw, k1_sb, DKW_TAG)
-                dwd = deal(nc.vector, "dwd", dkw, I32)
+                dwd = deal(nc.vector, "dwd", dkw, I32, "y_plain2")
 
         def by_pairs(rows):
             return rows.rearrange("p t (c i) -> p c t i", i=2)
@@ -203,18 +203,22 @@ def tile_picked_twqtriebstd_none_po_kernel(
             z_in = keep.tile([P, (hi - lo) * PACK], BF16, name="z_in%d" % lo, align_bytes=64)
             nc.vector.tensor_tensor(woven(z_in), by_pairs(v[:, :, lo:hi]), by_pairs(gate[:, :, lo:hi]), ALU.mult)
             nc.vector.quantize_mx(z_codes[:, lo:hi].bitcast(FP8X4), z_scales[:, lo:hi], z_in[:])
-            for t in range(PACK):
-                acc = bank(4, "h_last") if (hi, t) == (S, 0) else h_acc[t]
-                product(acc[:, lo:hi], dwd, dsd, t, z_codes[:, lo:hi], z_scales[:, lo:hi])
-                if (hi, t) in WCOPY:
-                    nc.scalar.activation(w_win[t][:, WCOPY[hi, t] : hi], acc[:, WCOPY[hi, t] : hi], ACT.Copy, scale=W_SCALE)
+            acc = bank(4, "h_last") if hi == S else h_acc[0]
+            product(acc[:, lo:hi], dwd, dsd, 0, z_codes[:, lo:hi], z_scales[:, lo:hi])
+            if hi in WCOPY:
+                nc.scalar.activation(w_win[0][:, WCOPY[hi] : hi], acc[:, WCOPY[hi] : hi], ACT.Copy, scale=W_SCALE)
+        for t in range(1, PACK):
+            product(h_acc[t][:], dwd, dsd, t, z_codes[:], z_scales[:])
+            nc.scalar.activation(w_win[t][:, :S], h_acc[t][:], ACT.Copy, scale=W_SCALE)
 
         result = keep.tile([P, PACK, S], F32, name="result", align_bytes=64)
         o_codes = keep.tile([P, S], I32, name="o_codes", align_bytes=64)
         o_scales = keep.tile([P, S], U8, name="o_scales", align_bytes=64)
         out_rows = out_0.rearrange("(p t) j -> p t j", t=PACK)
         units = UNITS
-        w_even = {}
+        spare = bank(7, "spare") if FILL0 else None
+        for k in range(FILL0):
+            nc.tensor.transpose(spare[:, chunk(k % 4)], w_win[FILL0_T][:, chunk(k % 4)], ident[:])
         for i, (t, lo, hi) in enumerate(units):
             n = hi - lo
             w = w_win[t]
@@ -247,6 +251,8 @@ def tile_picked_twqtriebstd_none_po_kernel(
                 for c in range(n // CH):
                     turn_and_add(diff[:, chunk(c)], [dif[:, chunk(c)]] if design == 20 else [both[:, chunk(c)], a[:, chunk(c)], a[:, chunk(c)]])
                 nc.scalar.activation(diff2[:], diff[:, :n], ACT.Square, scale=D_SCALE)
+                for k in range(FILL[i]):
+                    nc.tensor.transpose(spare[:, chunk(k % 4)], both[:, chunk(k % (n // CH))], ident[:])
                 for c in range(n // CH):
                     turn_and_add(total[:, chunk(c)], [diff2[:, chunk(c)], even2[:, chunk(c)]])
                 nc.scalar.activation(root[:], total[:, :n], ACT.Abs_reciprocal_sqrt, bias=0.25)

@@ -17,35 +17,19 @@ ALU = mybir.AluOpType
 ACT = mybir.ActivationFunctionType
 
 P = 128
-PACK = 4
-CH = 128
-PIECES = ((0, 256), (256, 384), (384, 512))
+SLOTS = 4
+HALF = S // 2
+HALVES = ((0, HALF), (HALF, S))
 
-WPACK = False
-GDEAL = True
-GOPS = ()
-GLAST = {"both":3,"diff":3,"out":2}
-BA = 2
-BB = 2
-BBOTH = 2
-BSQ = 3
-DESIGN = (20,20,20,20,20,20,20,20,0)
-SCAST = (0,)
-UNITS = [(0,0,256),(1,0,256),(2,0,256),(3,0,256),(0,256,512),(1,256,512),(2,256,512),(3,256,384),(3,384,512)]
-BANKS = [(5+i)%7 for i in range(40)]
-DKW_AT = 3
-DKW_TAG = "dkw"
-ZPIECES = ((0,256),(256,384),(384,512))
-WCOPY = {384:0,512:384}
-X1TAG = "x1w"
-FILL = (0,)*9
-FILL0 = 0
-FILL0_T = 1
 M = 0.3125
-KAPPA = -M
-W_SCALE = 0.0625 * KAPPA
-E_SCALE = (1.0 - 2.0 * M) / M / 2.0**0.5
-D_SCALE = 1.0 / M / 2.0**0.5
+RATIO = (1.0 - 2.0 * M) / (2.0 * M)
+KAPPA = M / RATIO
+H_SCALE = 0.0625
+EVEN_SCALE = 2.0 * M / KAPPA / 2.0**0.5
+DIFF_SCALE = 1.0 / M / 2.0**0.5
+
+UNITS = [(0, 0, S), (1, 0, S)] + [(t, lo, hi) for lo, hi in HALVES for t in (2, 3)]
+SHORT_CHAIN_UNITS = 2
 
 
 def tile_picked_twqtriebstd_none_po_kernel(
@@ -56,11 +40,17 @@ def tile_picked_twqtriebstd_none_po_kernel(
     with ExitStack() as ctx:
         lists = ctx.enter_context(tc.tile_pool(name="lists", bufs=1))
         keep = ctx.enter_context(tc.tile_pool(name="keep", bufs=1))
-        ring = ctx.enter_context(tc.tile_pool(name="ring", bufs=2))
+        ring = ctx.enter_context(tc.tile_pool(name="ring", bufs=4))
         psum = ctx.enter_context(tc.psum_pool(name="psum", bufs=1))
 
-        def bank(b, name):
-            return psum.tile([P, 512], F32, name=name, tag="bank%d" % b)
+        def bank(number, name):
+            return psum.tile([P, S], F32, name=name, tag="bank%d" % number)
+
+        def held(name, columns, dtype, tag=""):
+            return keep.tile([P, columns], dtype, name=name, tag=tag or name, align_bytes=64)
+
+        def passing(name, columns, dtype=F32):
+            return ring.tile([P, columns], dtype, name=name, align_bytes=64)
 
         def words_of(dram):
             return dram[0].rearrange("p n t -> p (n t)").bitcast(I32)
@@ -70,220 +60,196 @@ def tile_picked_twqtriebstd_none_po_kernel(
             nc.sync.dma_start(tile[:], dram)
             return tile
 
-        def cols16(tile, lo, hi):
-            return tile[:, lo // 16 : hi // 16]
+        def load_words(name, dram):
+            tile = held(name, dram.shape[2], I32)
+            nc.sync.dma_start(tile[:], words_of(dram))
+            return tile
 
-        xw = keep.tile([P, T], I32, name="xw", align_bytes=64)
-        xs = keep.tile([P, T], U8, name="xs", align_bytes=64)
-        w1w = keep.tile([P, H], I32, name="w1w", align_bytes=64)
-        w2w = keep.tile([P, H], I32, name="w2w", tag="w2w", align_bytes=64)
-        w1s = keep.tile([P, H], U8, name="w1s", align_bytes=64)
-        w2s = keep.tile([P, H], U8, name="w2s", tag="w2s", align_bytes=64)
-        ws = w2s if WPACK else None
-        dw = keep.tile([P, G], I32, name="dw", align_bytes=64)
-        ds = keep.tile([P, G], U8, name="ds", align_bytes=64)
-        gs_sb = keep.tile([P, PACK], F32, name="gs_sb")
-        ident = keep.tile([P, P], F32, name="ident", align_bytes=64)
-        warm = keep.tile([P, 2], F32, name="warm")
-
-        def load_scales(tile, dram):
+        def load_scales(name, dram, queues):
+            tile = held(name, dram.shape[2], U8)
             rows = dram[0].bitcast(I32)
             for r in range(4):
-                nc.sync.dma_start(
+                queues[r % len(queues)].dma_start(
                     tile[:].bitcast(I32)[r:P:4, :], rows[r:16:4, :].unsqueeze(1).broadcast_to([4, 8, rows.shape[1]])
                 )
+            return tile
 
-        nc.vector.memset(ds[:].bitcast(I32), 0)
-        nc.vector.memset(warm[:], 0.0)
-        make_identity(nc, ident[:])
+        def entries(offsets, lo, hi):
+            return offsets[:, lo // 16 : hi // 16]
 
-        two_sb = load_list("two_sb", two)
-        load_scales(xs, x_scales)
-        offs_sb = load_list("offs_sb", offs)
-        nc.sync.dma_start(xw[:], words_of(x_words))
-        nc.scalar.activation(warm[:, 1:2], warm[:, 0:1], ACT.Sigmoid)
-        nc.sync.dma_start(w2w[:], words_of(w2_words))
-        load_scales(w2s, w2_scales)
-        nc.sync.dma_start(w1w[:], words_of(w1_words))
-        load_scales(w1s, w1_scales)
-        k1_sb = load_list("k1_sb", k1)
-        for e in range(2):
-            nc.sync.dma_start(ds[:].bitcast(I32)[e:P:16, :], d_scales[0].bitcast(I32)[e:16:2, :])
-        n2_sb = load_list("n2_sb", n2)
-        nc.sync.dma_start(gs_sb[:], gs.rearrange("(p t) o -> p (t o)", t=PACK))
-        n1_sb = load_list("n1_sb", n1)
-        nc.sync.dma_start(dw[:], words_of(d_words))
-        n3_sb = load_list("n3_sb", n3)
-        n4_sb = load_list("n4_sb", n4)
-
-        def gather_words(name, table, offsets, tag):
-            picked = keep.tile([P, S], I32, name=name, tag=tag, align_bytes=64)
+        def gather_words(name, table, offsets):
+            picked = held(name, S, I32)
             nc.vector.tensor_copy(picked[:].bitcast(U32), table[:].bitcast(U32).indirect(offsets[:]))
             return picked
 
-        def gather_bytes(name, table, offsets, tag):
-            picked = keep.tile([P, S], U8, name=name, tag=tag, align_bytes=64)
+        def gather_bytes(name, table, offsets):
+            picked = held(name, S, U8)
             nc.vector.tensor_copy(picked[:], table[:].indirect(offsets[:]))
             return picked
 
-        def deal(engine, name, src, dtype, tag=""):
-            dealt = keep.tile([P, H], dtype, name=name, tag=tag or name, align_bytes=64)
-            engine.tensor_copy(
-                dealt[:].rearrange("p (t m) -> p t m", t=PACK), src[:].rearrange("p (m t) -> p t m", t=PACK)
-            )
+        def by_slot(matrix):
+            return matrix[:].rearrange("p (m t) -> p t m", t=SLOTS)
+
+        def deal(engine, name, matrix, dtype):
+            dealt = held(name, H, dtype)
+            engine.tensor_copy(dealt[:].rearrange("p (t m) -> p t m", t=SLOTS), by_slot(matrix))
             return dealt
 
-        def product(out, lhs, lhs_scale, t, rhs, rhs_scale):
-            cols = slice(t * P, (t + 1) * P)
+        def block(c):
+            return slice(c * P, (c + 1) * P)
+
+        def product(out, lhs, lhs_scale, rhs, rhs_scale):
             nc.tensor.matmul_mx(
-                out, lhsT=lhs[:, cols].bitcast(FP8X4), lhsT_scale=lhs_scale[:, cols],
+                out, lhsT=lhs.bitcast(FP8X4), lhsT_scale=lhs_scale,
                 rhs=rhs.bitcast(FP8X4), rhs_scale=rhs_scale, start=True, stop=True,
             )
 
-        def turn_and_add(out, sources):
-            for i, src in enumerate(sources):
-                nc.tensor.matmul(out, lhsT=src, rhs=ident[:], start=i == 0, stop=i == len(sources) - 1, is_transpose=True)
+        def turn_and_add(out, sources, columns):
+            for c in range(columns // P):
+                for i, source in enumerate(sources):
+                    nc.tensor.matmul(
+                        out[:, block(c)], lhsT=source[:, block(c)], rhs=identity[:],
+                        start=i == 0, stop=i == len(sources) - 1, is_transpose=True,
+                    )
 
-        def chunk(c):
-            return slice(c * CH, (c + 1) * CH)
-
-        dealer = nc.gpsimd if GDEAL else nc.vector
-        x2s = gather_bytes("x2s", xs, two_sb, "x2s")
-        x1s = gather_bytes("x1s", xs, offs_sb, "x1s")
-        x2w = gather_words("x2w", xw, two_sb, "x2w")
-        w2d = deal(dealer, "w2d", w2w, I32)
-        w2sd = deal(dealer, "w2sd", w2s, U8)
-        x1w = gather_words("x1w", xw, offs_sb, X1TAG)
-        dks = gather_bytes("dks", ds, k1_sb, "dks")
-        w1d = deal(dealer, "w1d", w1w, I32)
-        dsd = deal(nc.vector, "dsd", dks, U8)
-        for e in range(2):
-            nc.sync.dma_start(dsd[:].bitcast(I32)[2 + e : P : 32, :], dsd[:].bitcast(I32)[16 + e : P : 32, :])
-        w1sd = w2sd[4:P, :] if WPACK else deal(dealer, "w1sd", w1s, U8)
-
-        def windows(name, banks, lhs, lhs_scale, rhs, rhs_scale, scale):
-            pairs = []
-            for t in range(PACK):
-                acc = bank(banks + t, name + "_acc")
-                product(acc[:], lhs, lhs_scale, t, rhs[:], rhs_scale[:])
-                win = keep.tile([P, 2 * S], F32, name="%s_win%d" % (name, t), tag="%s_win%d" % (name, t), align_bytes=64)
-                plain = keep.tile([P, S], F32, name="%s_plain%d" % (name, t), tag="%s_plain%d" % (name, t), align_bytes=64)
-                for copy in (win[:, :S], plain[:]):
-                    nc.scalar.activation(copy, acc[:], ACT.Copy, scale=scale(t))
-                pairs.append((win, plain))
-            return pairs
-
-        d_pairs = windows("d", 0, w2d, w2sd, x2w, x2s, lambda t: 1.0)
-        y_pairs = windows("y", 4, w1d, w1sd, x1w, x1s, lambda t: gs_sb[:, t : t + 1])
-
-        gate = keep.tile([P, PACK, S], F32, name="gate", align_bytes=64)
-        for t, (win, plain) in enumerate(d_pairs):
-            u = ring.tile([P, S], F32, name="u", align_bytes=64, bufs=4)
-            nc.vector.tensor_tensor(u[:], win[:].indirect(n2_sb[:]), plain[:], ALU.add)
-            nc.scalar.activation(gate[:, t, :], u[:], ACT.Sigmoid)
-        nc.scalar.activation(warm[:, 1:2], gate[:, PACK - 1, 0:1], ACT.Abs_reciprocal_sqrt)
-        v = keep.tile([P, PACK, S], F32, name="v", align_bytes=64)
-        for t, (win, plain) in enumerate(y_pairs):
-            nc.vector.tensor_tensor(v[:, t, :], win[:].indirect(n1_sb[:]), plain[:], ALU.add)
-            if t == DKW_AT:
-                dkw = gather_words("dkw", dw, k1_sb, DKW_TAG)
-                dwd = deal(nc.vector, "dwd", dkw, I32, "y_plain2")
-
-        def by_pairs(rows):
+        def column_pairs(rows):
             return rows.rearrange("p t (c i) -> p c t i", i=2)
 
-        def woven(tile):
-            return tile[:].rearrange("p (c i t) -> p c t i", i=2, t=PACK)
+        def interleaved(tile):
+            return tile[:].rearrange("p (c i t) -> p c t i", i=2, t=SLOTS)
 
-        z_codes = keep.tile([P, S], I32, name="z_codes", align_bytes=64)
-        z_scales = keep.tile([P, S], U8, name="z_scales", align_bytes=64)
-        h_acc = [bank(t, "h_acc") for t in range(PACK)]
-        w_win = [keep.tile([P, 2 * S if (t, 0, S) in UNITS else S], F32, name="w_win%d" % t, align_bytes=64) for t in range(PACK)]
-        for lo, hi in ZPIECES:
-            z_in = keep.tile([P, (hi - lo) * PACK], BF16, name="z_in%d" % lo, align_bytes=64)
-            nc.vector.tensor_tensor(woven(z_in), by_pairs(v[:, :, lo:hi]), by_pairs(gate[:, :, lo:hi]), ALU.mult)
-            nc.vector.quantize_mx(z_codes[:, lo:hi].bitcast(FP8X4), z_scales[:, lo:hi], z_in[:])
-            acc = bank(4, "h_last") if hi == S else h_acc[0]
-            product(acc[:, lo:hi], dwd, dsd, 0, z_codes[:, lo:hi], z_scales[:, lo:hi])
-            if hi in WCOPY:
-                nc.scalar.activation(w_win[0][:, WCOPY[hi] : hi], acc[:, WCOPY[hi] : hi], ACT.Copy, scale=W_SCALE)
-        for t in range(1, PACK):
-            product(h_acc[t][:], dwd, dsd, t, z_codes[:], z_scales[:])
-            nc.scalar.activation(w_win[t][:, :S], h_acc[t][:], ACT.Copy, scale=W_SCALE)
+        d_bytes = held("d_bytes", G, U8)
+        nc.vector.memset(d_bytes[:].bitcast(I32), 0)
+        identity = held("identity", P, F32)
+        make_identity(nc, identity[:])
 
-        result = keep.tile([P, PACK, S], F32, name="result", align_bytes=64)
-        o_codes = keep.tile([P, S], I32, name="o_codes", align_bytes=64)
-        o_scales = keep.tile([P, S], U8, name="o_scales", align_bytes=64)
-        out_rows = out_0.rearrange("(p t) j -> p t j", t=PACK)
-        units = UNITS
-        spare = bank(7, "spare") if FILL0 else None
-        for k in range(FILL0):
-            nc.tensor.transpose(spare[:, chunk(k % 4)], w_win[FILL0_T][:, chunk(k % 4)], ident[:])
-        for i, (t, lo, hi) in enumerate(units):
+        two_sb = load_list("two_sb", two)
+        x_bytes = load_scales("x_bytes", x_scales, (nc.scalar, nc.sync))
+        offs_sb = load_list("offs_sb", offs)
+        x_table = load_words("x_table", x_words)
+        w2_codes = load_words("w2_codes", w2_words)
+        w2_bytes = load_scales("w2_bytes", w2_scales, (nc.sync,))
+        w1_codes = load_words("w1_codes", w1_words)
+        w1_bytes = load_scales("w1_bytes", w1_scales, (nc.sync,))
+        k1_sb = load_list("k1_sb", k1)
+        for e in range(2):
+            nc.sync.dma_start(d_bytes[:].bitcast(I32)[e:P:16, :], d_scales[0].bitcast(I32)[e:16:2, :])
+        n2_sb = load_list("n2_sb", n2)
+        gs_sb = held("gs_sb", SLOTS, F32)
+        nc.sync.dma_start(gs_sb[:], gs.rearrange("(p t) o -> p (t o)", t=SLOTS))
+        n1_sb = load_list("n1_sb", n1)
+        d_table = load_words("d_table", d_words)
+        n3_sb = load_list("n3_sb", n3)
+        n4_sb = load_list("n4_sb", n4)
+
+        two_scales = gather_bytes("two_scales", x_bytes, two_sb)
+        offs_scales = gather_bytes("offs_scales", x_bytes, offs_sb)
+        two_codes = gather_words("two_codes", x_table, two_sb)
+        w2_dealt = deal(nc.gpsimd, "w2_dealt", w2_codes, I32)
+        w2_scales_dealt = deal(nc.gpsimd, "w2_scales_dealt", w2_bytes, U8)
+        offs_codes = gather_words("offs_codes", x_table, offs_sb)
+        k1_scales = gather_bytes("k1_scales", d_bytes, k1_sb)
+        w1_dealt = deal(nc.gpsimd, "w1_dealt", w1_codes, I32)
+        k1_scales_dealt = deal(nc.vector, "k1_scales_dealt", k1_scales, U8)
+        for e in range(2):
+            rows = k1_scales_dealt[:].bitcast(I32)
+            nc.sync.dma_start(rows[2 + e : P : 32, :], rows[16 + e : P : 32, :])
+        w1_scales_dealt = deal(nc.gpsimd, "w1_scales_dealt", w1_bytes, U8)
+
+        def project(name, first_bank, lhs, lhs_scale, rhs, rhs_scale, row_scale):
+            pairs = []
+            for t in range(SLOTS):
+                sums = bank(first_bank + t, name + "_sums")
+                product(sums[:], lhs[:, block(t)], lhs_scale[:, block(t)], rhs[:], rhs_scale[:])
+                window = held("%s_window%d" % (name, t), 2 * S, F32)
+                plain = held("%s_plain%d" % (name, t), S, F32)
+                for copy in (window[:, :S], plain[:]):
+                    nc.scalar.activation(copy, sums[:], ACT.Copy, scale=row_scale(t))
+                pairs.append((window, plain))
+            return pairs
+
+        d_pairs = project("d", 0, w2_dealt, w2_scales_dealt, two_codes, two_scales, lambda t: 1.0)
+        y_pairs = project("y", SLOTS, w1_dealt, w1_scales_dealt, offs_codes, offs_scales, lambda t: gs_sb[:, t : t + 1])
+
+        gate = keep.tile([P, SLOTS, S], F32, name="gate", align_bytes=64)
+        d_sum = keep.tile([P, SLOTS, S], F32, name="d_sum", align_bytes=64)
+        for t, (window, plain) in enumerate(d_pairs):
+            nc.vector.tensor_tensor(d_sum[:, t, :], window[:].indirect(n2_sb[:]), plain[:], ALU.add)
+        for lo, hi in HALVES:
+            nc.scalar.activation(gate[:, :, lo:hi], d_sum[:, :, lo:hi], ACT.Sigmoid)
+        y_sum = keep.tile([P, SLOTS, S], F32, name="y_sum", align_bytes=64)
+        for t, (window, plain) in enumerate(y_pairs):
+            nc.vector.tensor_tensor(y_sum[:, t, :], window[:].indirect(n1_sb[:]), plain[:], ALU.add)
+
+        k1_codes = gather_words("k1_codes", d_table, k1_sb)
+        k1_slot0 = held("k1_slot0", P, I32)
+        nc.vector.tensor_copy(k1_slot0[:], by_slot(k1_codes)[:, 0, :])
+
+        z_codes = held("z_codes", S, I32)
+        z_scales = held("z_scales", S, U8)
+        h_sums = [bank(t, "h_sums") for t in range(SLOTS)]
+        h0_sums = (h_sums[0], bank(SLOTS, "h0_right"))
+        w_window = [held("w_window%d" % t, 2 * S if (t, 0, S) in UNITS else S, F32) for t in range(SLOTS)]
+        for sums, (lo, hi) in zip(h0_sums, HALVES):
+            z_bf16 = held("z_bf16_%d" % lo, HALF * SLOTS, BF16)
+            nc.vector.tensor_tensor(
+                interleaved(z_bf16), column_pairs(y_sum[:, :, lo:hi]), column_pairs(gate[:, :, lo:hi]), ALU.mult
+            )
+            nc.vector.quantize_mx(z_codes[:, lo:hi].bitcast(FP8X4), z_scales[:, lo:hi], z_bf16[:])
+            product(sums[:, lo:hi], k1_slot0[:], k1_scales_dealt[:, block(0)], z_codes[:, lo:hi], z_scales[:, lo:hi])
+            nc.scalar.activation(w_window[0][:, lo:hi], sums[:, lo:hi], ACT.Copy, scale=H_SCALE * KAPPA)
+        k1_rest = held("k1_rest", H, I32, tag="z_bf16_%d" % HALF)
+        nc.vector.tensor_copy(k1_rest[:].rearrange("p (t m) -> p t m", t=SLOTS)[:, 1:, :], by_slot(k1_codes)[:, 1:, :])
+        for t in range(1, SLOTS):
+            product(h_sums[t][:], k1_rest[:, block(t)], k1_scales_dealt[:, block(t)], z_codes[:], z_scales[:])
+            nc.scalar.activation(w_window[t][:, :S], h_sums[t][:], ACT.Copy, scale=H_SCALE * KAPPA)
+
+        result = keep.tile([P, SLOTS, S], F32, name="result", align_bytes=64)
+        out_codes = held("out_codes", S, I32)
+        out_scales = held("out_scales", S, U8)
+        out_rows = out_0.rearrange("(p t) j -> p t j", t=SLOTS)
+        for i, (t, lo, hi) in enumerate(UNITS):
             n = hi - lo
-            w = w_win[t]
-            design = DESIGN[i]
-            eng = {k: nc.gpsimd if k in GOPS and t < GLAST[k] else nc.vector for k in ("both", "diff", "out")}
-            a = ring.tile([P, n], F32, name="a", align_bytes=64, bufs=BA)
-            both = ring.tile([P, n], F32, name="both", align_bytes=64, bufs=BBOTH)
-            num = ring.tile([P, n], F32, name="num", align_bytes=64, bufs=3)
-            dif = ring.tile([P, n], F32, name="dif", align_bytes=64)
-            diff2 = ring.tile([P, n], F32, name="diff2", align_bytes=64, bufs=BSQ)
-            even2 = ring.tile([P, n], F32, name="even2", align_bytes=64, bufs=BSQ)
-            root = ring.tile([P, n], F32, name="root", align_bytes=64)
-            nc.vector.tensor_scalar(a[:], w[:].indirect(cols16(n3_sb, lo, hi)), -1.0, 0.0, ALU.mult, ALU.add)
-            nc.vector.tensor_tensor(both[:], w[:].indirect(cols16(n4_sb, lo, hi)), a[:], ALU.subtract)
-            if design <= 20:
-                nc.vector.scalar_tensor_tensor(dif[:], a[:], 2.0, both[:], ALU.mult, ALU.add)
-            if design <= 12:
-                ev = ring.tile([P, n], F32, name="ev", align_bytes=64)
-                nc.vector.scalar_tensor_tensor(ev[:], w[:, lo:hi], -5.0 / 3.0, both[:], ALU.mult, ALU.add)
-            nc.vector.scalar_tensor_tensor(num[:], w[:, lo:hi], -2.2, both[:], ALU.mult, ALU.add)
-            if design >= 20:
-                we = ring.tile([P, n], F32, name="we", align_bytes=64)
-                nc.scalar.activation(we[:], w[:, lo:hi], ACT.Copy, scale=-5.0 / 3.0)
-                diff = bank(BANKS[3 * i], "diff")
-                even = bank(BANKS[3 * i + 1], "even")
-                total = bank(BANKS[3 * i + 2], "total")
-                for c in range(n // CH):
-                    turn_and_add(even[:, chunk(c)], [both[:, chunk(c)], we[:, chunk(c)]])
-                nc.scalar.activation(even2[:], even[:, :n], ACT.Square, scale=E_SCALE)
-                for c in range(n // CH):
-                    turn_and_add(diff[:, chunk(c)], [dif[:, chunk(c)]] if design == 20 else [both[:, chunk(c)], a[:, chunk(c)], a[:, chunk(c)]])
-                nc.scalar.activation(diff2[:], diff[:, :n], ACT.Square, scale=D_SCALE)
-                for k in range(FILL[i]):
-                    nc.tensor.transpose(spare[:, chunk(k % 4)], both[:, chunk(k % (n // CH))], ident[:])
-                for c in range(n // CH):
-                    turn_and_add(total[:, chunk(c)], [diff2[:, chunk(c)], even2[:, chunk(c)]])
-                nc.scalar.activation(root[:], total[:, :n], ACT.Abs_reciprocal_sqrt, bias=0.25)
-                eng["out"].tensor_tensor(result[:, t, lo:hi], num[:], root[:], ALU.mult)
-            else:
-                nc.scalar.activation(diff2[:], dif[:], ACT.Square, scale=D_SCALE)
-                nc.scalar.activation(even2[:], ev[:], ACT.Square, scale=E_SCALE)
-                if design == 12:
-                    total = bank(BANKS[3 * i], "total")
-                    rback = bank(BANKS[3 * i + 1], "rback")
-                    for c in range(n // CH):
-                        turn_and_add(total[:, chunk(c)], [even2[:, chunk(c)], diff2[:, chunk(c)]])
-                    nc.scalar.activation(root[:], total[:, :n], ACT.Abs_reciprocal_sqrt, bias=0.25)
-                    for c in range(n // CH):
-                        turn_and_add(rback[:, chunk(c)], [root[:, chunk(c)]])
-                    nc.vector.tensor_tensor(result[:, t, lo:hi], rback[:, :n], num[:], ALU.mult)
-                else:
-                    tot = ring.tile([P, n], F32, name="tot", align_bytes=64)
-                    nc.vector.tensor_tensor(tot[:], even2[:], diff2[:], ALU.add)
-                    nc.scalar.activation(root[:], tot[:], ACT.Abs_reciprocal_sqrt, bias=0.25)
-                    nc.vector.tensor_tensor(result[:, t, lo:hi], num[:], root[:], ALU.mult)
-            nc.sync.dma_start(out_rows[:, t, lo:hi], result[:, t, lo:hi])
-            if t == PACK - 1:
-                o_in = ring.tile([P, n * PACK], BF16, name="o_in", align_bytes=64, bufs=3)
-                if lo in SCAST:
-                    nc.scalar.copy(woven(o_in), by_pairs(result[:, :, lo:hi]))
-                else:
-                    nc.vector.tensor_copy(woven(o_in), by_pairs(result[:, :, lo:hi]))
-                nc.vector.quantize_mx(
-                    o_codes[:, lo:hi].bitcast(FP8X4), o_scales[:, lo:hi], o_in[:]
+            window = w_window[t]
+            a, b, minus, plus = (passing(name, n) for name in ("a", "b", "minus", "plus"))
+            even2, diff2, root = (passing(name, n) for name in ("even2", "diff2", "root"))
+            centred = held("centred%d" % i, n, F32)
+            nc.vector.tensor_scalar(a[:], window[:].indirect(entries(n3_sb, lo, hi)), -RATIO, 0.0, ALU.mult, ALU.add)
+            nc.vector.tensor_scalar(b[:], window[:].indirect(entries(n4_sb, lo, hi)), RATIO, 0.0, ALU.mult, ALU.add)
+            nc.gpsimd.tensor_tensor(minus[:], a[:], b[:], ALU.subtract)
+            nc.gpsimd.tensor_tensor(plus[:], a[:], b[:], ALU.add)
+            h_parts = zip(h0_sums, HALVES) if t == 0 else [(h_sums[t], (lo, hi))]
+            for sums, (c0, c1) in h_parts:
+                nc.vector.scalar_tensor_tensor(
+                    centred[:, c0 - lo : c1 - lo], sums[:, c0:c1], H_SCALE * (1.0 - M), minus[:, c0 - lo : c1 - lo],
+                    ALU.mult, ALU.add,
                 )
-                nc.sync.dma_start(words_of(out_1)[:, lo:hi], o_codes[:, lo:hi])
+            if i < len(UNITS) - SHORT_CHAIN_UNITS:
+                diff, even, total = bank(5, "diff"), bank(6, "even"), bank(7, "total")
+                turn_and_add(even, [minus, window[:, lo:hi]], n)
+                nc.scalar.activation(even2[:], even[:, :n], ACT.Square, scale=EVEN_SCALE)
+                turn_and_add(diff, [plus], n)
+                nc.scalar.activation(diff2[:], diff[:, :n], ACT.Square, scale=DIFF_SCALE)
+                turn_and_add(total, [diff2, even2], n)
+            else:
+                even, total = passing("even", n), passing("total", n)
+                nc.vector.scalar_tensor_tensor(
+                    even[:], h_sums[t][:, lo:hi], H_SCALE * KAPPA, minus[:], ALU.mult, ALU.add
+                )
+                nc.scalar.activation(even2[:], even[:], ACT.Square, scale=EVEN_SCALE)
+                nc.scalar.activation(diff2[:], plus[:], ACT.Square, scale=DIFF_SCALE)
+                nc.vector.tensor_tensor(total[:], even2[:], diff2[:], ALU.add)
+            nc.scalar.activation(root[:], total[:, :n], ACT.Abs_reciprocal_sqrt, bias=0.25)
+            nc.vector.tensor_tensor(result[:, t, lo:hi], centred[:], root[:], ALU.mult)
+            nc.sync.dma_start(out_rows[:, t, lo:hi], result[:, t, lo:hi])
+            if t == SLOTS - 1:
+                out_bf16 = passing("out_bf16", n * SLOTS, BF16)
+                pairs = n // 4
+                nc.scalar.copy(interleaved(out_bf16)[:, :pairs], column_pairs(result[:, :, lo:hi])[:, :pairs])
+                nc.vector.tensor_copy(interleaved(out_bf16)[:, pairs:], column_pairs(result[:, :, lo:hi])[:, pairs:])
+                nc.vector.quantize_mx(out_codes[:, lo:hi].bitcast(FP8X4), out_scales[:, lo:hi], out_bf16[:])
+                nc.sync.dma_start(words_of(out_1)[:, lo:hi], out_codes[:, lo:hi])
         for q in range(4):
-            (nc.scalar if q % 2 else nc.sync).dma_start(out_2[0].bitcast(I32)[4 * q : 4 * q + 4, :], o_scales[:].bitcast(I32)[32 * q : 32 * q + 4, :])
+            (nc.sync, nc.scalar)[q % 2].dma_start(
+                out_2[0].bitcast(I32)[4 * q : 4 * q + 4, :], out_scales[:].bitcast(I32)[32 * q : 32 * q + 4, :]
+            )

@@ -3,7 +3,7 @@ from contextlib import ExitStack
 import concourse.mybir as mybir
 from concourse.masks import make_identity
 
-K, T, S, H, G = 512, 1024, 512, 512, 2048
+K, S, H, G = 512, 512, 512, 2048
 FLOPS = 3 * 2 * K * H * S
 
 F32 = mybir.dt.float32
@@ -29,7 +29,8 @@ EVEN_SCALE = 2.0 * M / KAPPA / 2.0**0.5
 DIFF_SCALE = 1.0 / M / 2.0**0.5
 
 UNITS = [(0, 0, S), (1, 0, S)] + [(t, lo, hi) for lo, hi in HALVES for t in (2, 3)]
-SHORT_CHAIN_UNITS = 2
+SHORT_CHAIN_UNITS = 3
+GPSIMD_CENTRED_UNITS = 1
 
 
 def tile_picked_twqtriebstd_none_po_kernel(
@@ -151,9 +152,9 @@ def tile_picked_twqtriebstd_none_po_kernel(
         k1_scales = gather_bytes("k1_scales", d_bytes, k1_sb)
         w1_dealt = deal(nc.gpsimd, "w1_dealt", w1_codes, I32)
         k1_scales_dealt = deal(nc.vector, "k1_scales_dealt", k1_scales, U8)
+        k1_rows = k1_scales_dealt[:].bitcast(I32)
         for e in range(2):
-            rows = k1_scales_dealt[:].bitcast(I32)
-            nc.sync.dma_start(rows[2 + e : P : 32, :], rows[16 + e : P : 32, :])
+            nc.sync.dma_start(k1_rows[2 + e : P : 32, :], k1_rows[16 + e : P : 32, :])
         w1_scales_dealt = deal(nc.gpsimd, "w1_scales_dealt", w1_bytes, U8)
 
         def project(name, first_bank, lhs, lhs_scale, rhs, rhs_scale, row_scale):
@@ -211,26 +212,31 @@ def tile_picked_twqtriebstd_none_po_kernel(
         for i, (t, lo, hi) in enumerate(UNITS):
             n = hi - lo
             window = w_window[t]
-            a, b, minus, plus = (passing(name, n) for name in ("a", "b", "minus", "plus"))
+            a, b, minus = (passing(name, n) for name in ("a", "b", "minus"))
             even2, diff2, root = (passing(name, n) for name in ("even2", "diff2", "root"))
             centred = held("centred%d" % i, n, F32)
             nc.vector.tensor_scalar(a[:], window[:].indirect(entries(n3_sb, lo, hi)), -RATIO, 0.0, ALU.mult, ALU.add)
             nc.vector.tensor_scalar(b[:], window[:].indirect(entries(n4_sb, lo, hi)), RATIO, 0.0, ALU.mult, ALU.add)
             nc.gpsimd.tensor_tensor(minus[:], a[:], b[:], ALU.subtract)
-            nc.gpsimd.tensor_tensor(plus[:], a[:], b[:], ALU.add)
-            h_parts = zip(h0_sums, HALVES) if t == 0 else [(h_sums[t], (lo, hi))]
-            for sums, (c0, c1) in h_parts:
+            by_transposes = i < len(UNITS) - SHORT_CHAIN_UNITS
+            if not by_transposes:
+                plus = passing("plus", n)
+                nc.gpsimd.tensor_tensor(plus[:], a[:], b[:], ALU.add)
+            if i < GPSIMD_CENTRED_UNITS:
+                h_part = passing("h_part", n)
+                nc.scalar.activation(h_part[:], window[:, lo:hi], ACT.Copy, scale=(1.0 - M) / KAPPA)
+                nc.gpsimd.tensor_tensor(centred[:], h_part[:], minus[:], ALU.add)
+            else:
                 nc.vector.scalar_tensor_tensor(
-                    centred[:, c0 - lo : c1 - lo], sums[:, c0:c1], H_SCALE * (1.0 - M), minus[:, c0 - lo : c1 - lo],
-                    ALU.mult, ALU.add,
+                    centred[:], h_sums[t][:, lo:hi], H_SCALE * (1.0 - M), minus[:], ALU.mult, ALU.add
                 )
-            if i < len(UNITS) - SHORT_CHAIN_UNITS:
+            if by_transposes:
                 diff, even, total = bank(5, "diff"), bank(6, "even"), bank(7, "total")
+                turn_and_add(diff, [b, a], n)
+                nc.scalar.activation(diff2[:], diff[:, :n], ACT.Square, scale=DIFF_SCALE)
                 turn_and_add(even, [minus, window[:, lo:hi]], n)
                 nc.scalar.activation(even2[:], even[:, :n], ACT.Square, scale=EVEN_SCALE)
-                turn_and_add(diff, [plus], n)
-                nc.scalar.activation(diff2[:], diff[:, :n], ACT.Square, scale=DIFF_SCALE)
-                turn_and_add(total, [diff2, even2], n)
+                turn_and_add(total, [even2, diff2], n)
             else:
                 even, total = passing("even", n), passing("total", n)
                 nc.vector.scalar_tensor_tensor(

from contextlib import ExitStack

import concourse.mybir as mybir
from concourse.masks import make_identity

K, S, H, G = 512, 512, 512, 2048
FLOPS = 3 * 2 * K * H * S

F32 = mybir.dt.float32
BF16 = mybir.dt.bfloat16
I32 = mybir.dt.int32
U32 = mybir.dt.uint32
U16 = mybir.dt.uint16
U8 = mybir.dt.uint8
FP8X4 = mybir.dt.float8_e4m3fn_x4
ALU = mybir.AluOpType
ACT = mybir.ActivationFunctionType

P = 128
SLOTS = 4
HALF = S // 2
HALVES = ((0, HALF), (HALF, S))

M = 0.3125
RATIO = (1.0 - 2.0 * M) / (2.0 * M)
KAPPA = M / RATIO
H_SCALE = 0.0625
EVEN_SCALE = 2.0 * M / KAPPA / 2.0**0.5
DIFF_SCALE = 1.0 / M / 2.0**0.5

UNITS = [(0, 0, S), (1, 0, S)] + [(t, lo, hi) for lo, hi in HALVES for t in (2, 3)]
SHORT_CHAIN_UNITS = 3
GPSIMD_CENTRED_UNITS = 1


def tile_picked_twqtriebstd_none_po_kernel(
    tc, x_words, x_scales, w1_words, w1_scales, w2_words, w2_scales, gs, d_words, d_scales,
    offs, two, n1, n2, k1, n3, n4, out_0, out_1, out_2,
):
    nc = tc.nc
    with ExitStack() as ctx:
        lists = ctx.enter_context(tc.tile_pool(name="lists", bufs=1))
        keep = ctx.enter_context(tc.tile_pool(name="keep", bufs=1))
        ring = ctx.enter_context(tc.tile_pool(name="ring", bufs=4))
        psum = ctx.enter_context(tc.psum_pool(name="psum", bufs=1))

        def bank(number, name):
            return psum.tile([P, S], F32, name=name, tag="bank%d" % number)

        def held(name, columns, dtype, tag=""):
            return keep.tile([P, columns], dtype, name=name, tag=tag or name, align_bytes=64)

        def passing(name, columns, dtype=F32):
            return ring.tile([P, columns], dtype, name=name, align_bytes=64)

        def words_of(dram):
            return dram[0].rearrange("p n t -> p (n t)").bitcast(I32)

        def load_list(name, dram):
            tile = lists.tile([P, S // 16], U16, name=name)
            nc.sync.dma_start(tile[:], dram)
            return tile

        def load_words(name, dram):
            tile = held(name, dram.shape[2], I32)
            nc.sync.dma_start(tile[:], words_of(dram))
            return tile

        def load_scales(name, dram, queues):
            tile = held(name, dram.shape[2], U8)
            rows = dram[0].bitcast(I32)
            for r in range(4):
                queues[r % len(queues)].dma_start(
                    tile[:].bitcast(I32)[r:P:4, :], rows[r:16:4, :].unsqueeze(1).broadcast_to([4, 8, rows.shape[1]])
                )
            return tile

        def entries(offsets, lo, hi):
            return offsets[:, lo // 16 : hi // 16]

        def gather_words(name, table, offsets):
            picked = held(name, S, I32)
            nc.vector.tensor_copy(picked[:].bitcast(U32), table[:].bitcast(U32).indirect(offsets[:]))
            return picked

        def gather_bytes(name, table, offsets):
            picked = held(name, S, U8)
            nc.vector.tensor_copy(picked[:], table[:].indirect(offsets[:]))
            return picked

        def by_slot(matrix):
            return matrix[:].rearrange("p (m t) -> p t m", t=SLOTS)

        def deal(engine, name, matrix, dtype):
            dealt = held(name, H, dtype)
            engine.tensor_copy(dealt[:].rearrange("p (t m) -> p t m", t=SLOTS), by_slot(matrix))
            return dealt

        def block(c):
            return slice(c * P, (c + 1) * P)

        def product(out, lhs, lhs_scale, rhs, rhs_scale):
            nc.tensor.matmul_mx(
                out, lhsT=lhs.bitcast(FP8X4), lhsT_scale=lhs_scale,
                rhs=rhs.bitcast(FP8X4), rhs_scale=rhs_scale, start=True, stop=True,
            )

        def turn_and_add(out, sources, columns):
            for c in range(columns // P):
                for i, source in enumerate(sources):
                    nc.tensor.matmul(
                        out[:, block(c)], lhsT=source[:, block(c)], rhs=identity[:],
                        start=i == 0, stop=i == len(sources) - 1, is_transpose=True,
                    )

        def column_pairs(rows):
            return rows.rearrange("p t (c i) -> p c t i", i=2)

        def interleaved(tile):
            return tile[:].rearrange("p (c i t) -> p c t i", i=2, t=SLOTS)

        d_bytes = held("d_bytes", G, U8)
        nc.vector.memset(d_bytes[:].bitcast(I32), 0)
        identity = held("identity", P, F32)
        make_identity(nc, identity[:])

        two_sb = load_list("two_sb", two)
        x_bytes = load_scales("x_bytes", x_scales, (nc.scalar, nc.sync))
        offs_sb = load_list("offs_sb", offs)
        x_table = load_words("x_table", x_words)
        w2_codes = load_words("w2_codes", w2_words)
        w2_bytes = load_scales("w2_bytes", w2_scales, (nc.sync,))
        w1_codes = load_words("w1_codes", w1_words)
        w1_bytes = load_scales("w1_bytes", w1_scales, (nc.sync,))
        k1_sb = load_list("k1_sb", k1)
        for e in range(2):
            nc.sync.dma_start(d_bytes[:].bitcast(I32)[e:P:16, :], d_scales[0].bitcast(I32)[e:16:2, :])
        n2_sb = load_list("n2_sb", n2)
        gs_sb = held("gs_sb", SLOTS, F32)
        nc.sync.dma_start(gs_sb[:], gs.rearrange("(p t) o -> p (t o)", t=SLOTS))
        n1_sb = load_list("n1_sb", n1)
        d_table = load_words("d_table", d_words)
        n3_sb = load_list("n3_sb", n3)
        n4_sb = load_list("n4_sb", n4)

        two_scales = gather_bytes("two_scales", x_bytes, two_sb)
        offs_scales = gather_bytes("offs_scales", x_bytes, offs_sb)
        two_codes = gather_words("two_codes", x_table, two_sb)
        w2_dealt = deal(nc.gpsimd, "w2_dealt", w2_codes, I32)
        w2_scales_dealt = deal(nc.gpsimd, "w2_scales_dealt", w2_bytes, U8)
        offs_codes = gather_words("offs_codes", x_table, offs_sb)
        k1_scales = gather_bytes("k1_scales", d_bytes, k1_sb)
        w1_dealt = deal(nc.gpsimd, "w1_dealt", w1_codes, I32)
        k1_scales_dealt = deal(nc.vector, "k1_scales_dealt", k1_scales, U8)
        k1_rows = k1_scales_dealt[:].bitcast(I32)
        for e in range(2):
            nc.sync.dma_start(k1_rows[2 + e : P : 32, :], k1_rows[16 + e : P : 32, :])
        w1_scales_dealt = deal(nc.gpsimd, "w1_scales_dealt", w1_bytes, U8)

        def project(name, first_bank, lhs, lhs_scale, rhs, rhs_scale, row_scale):
            pairs = []
            for t in range(SLOTS):
                sums = bank(first_bank + t, name + "_sums")
                product(sums[:], lhs[:, block(t)], lhs_scale[:, block(t)], rhs[:], rhs_scale[:])
                window = held("%s_window%d" % (name, t), 2 * S, F32)
                plain = held("%s_plain%d" % (name, t), S, F32)
                for copy in (window[:, :S], plain[:]):
                    nc.scalar.activation(copy, sums[:], ACT.Copy, scale=row_scale(t))
                pairs.append((window, plain))
            return pairs

        d_pairs = project("d", 0, w2_dealt, w2_scales_dealt, two_codes, two_scales, lambda t: 1.0)
        y_pairs = project("y", SLOTS, w1_dealt, w1_scales_dealt, offs_codes, offs_scales, lambda t: gs_sb[:, t : t + 1])

        gate = keep.tile([P, SLOTS, S], F32, name="gate", align_bytes=64)
        d_sum = keep.tile([P, SLOTS, S], F32, name="d_sum", align_bytes=64)
        for t, (window, plain) in enumerate(d_pairs):
            nc.vector.tensor_tensor(d_sum[:, t, :], window[:].indirect(n2_sb[:]), plain[:], ALU.add)
        for lo, hi in HALVES:
            nc.scalar.activation(gate[:, :, lo:hi], d_sum[:, :, lo:hi], ACT.Sigmoid)
        y_sum = keep.tile([P, SLOTS, S], F32, name="y_sum", align_bytes=64)
        for t, (window, plain) in enumerate(y_pairs):
            nc.vector.tensor_tensor(y_sum[:, t, :], window[:].indirect(n1_sb[:]), plain[:], ALU.add)

        k1_codes = gather_words("k1_codes", d_table, k1_sb)
        k1_slot0 = held("k1_slot0", P, I32)
        nc.vector.tensor_copy(k1_slot0[:], by_slot(k1_codes)[:, 0, :])

        z_codes = held("z_codes", S, I32)
        z_scales = held("z_scales", S, U8)
        h_sums = [bank(t, "h_sums") for t in range(SLOTS)]
        h0_sums = (h_sums[0], bank(SLOTS, "h0_right"))
        w_window = [held("w_window%d" % t, 2 * S if (t, 0, S) in UNITS else S, F32) for t in range(SLOTS)]
        for sums, (lo, hi) in zip(h0_sums, HALVES):
            z_bf16 = held("z_bf16_%d" % lo, HALF * SLOTS, BF16)
            nc.vector.tensor_tensor(
                interleaved(z_bf16), column_pairs(y_sum[:, :, lo:hi]), column_pairs(gate[:, :, lo:hi]), ALU.mult
            )
            nc.vector.quantize_mx(z_codes[:, lo:hi].bitcast(FP8X4), z_scales[:, lo:hi], z_bf16[:])
            product(sums[:, lo:hi], k1_slot0[:], k1_scales_dealt[:, block(0)], z_codes[:, lo:hi], z_scales[:, lo:hi])
            nc.scalar.activation(w_window[0][:, lo:hi], sums[:, lo:hi], ACT.Copy, scale=H_SCALE * KAPPA)
        k1_rest = held("k1_rest", H, I32, tag="z_bf16_%d" % HALF)
        nc.vector.tensor_copy(k1_rest[:].rearrange("p (t m) -> p t m", t=SLOTS)[:, 1:, :], by_slot(k1_codes)[:, 1:, :])
        for t in range(1, SLOTS):
            product(h_sums[t][:], k1_rest[:, block(t)], k1_scales_dealt[:, block(t)], z_codes[:], z_scales[:])
            nc.scalar.activation(w_window[t][:, :S], h_sums[t][:], ACT.Copy, scale=H_SCALE * KAPPA)

        result = keep.tile([P, SLOTS, S], F32, name="result", align_bytes=64)
        out_codes = held("out_codes", S, I32)
        out_scales = held("out_scales", S, U8)
        out_rows = out_0.rearrange("(p t) j -> p t j", t=SLOTS)
        for i, (t, lo, hi) in enumerate(UNITS):
            n = hi - lo
            window = w_window[t]
            a, b, minus = (passing(name, n) for name in ("a", "b", "minus"))
            even2, diff2, root = (passing(name, n) for name in ("even2", "diff2", "root"))
            centred = held("centred%d" % i, n, F32)
            nc.vector.tensor_scalar(a[:], window[:].indirect(entries(n3_sb, lo, hi)), -RATIO, 0.0, ALU.mult, ALU.add)
            nc.vector.tensor_scalar(b[:], window[:].indirect(entries(n4_sb, lo, hi)), RATIO, 0.0, ALU.mult, ALU.add)
            nc.gpsimd.tensor_tensor(minus[:], a[:], b[:], ALU.subtract)
            by_transposes = i < len(UNITS) - SHORT_CHAIN_UNITS
            if not by_transposes:
                plus = passing("plus", n)
                nc.gpsimd.tensor_tensor(plus[:], a[:], b[:], ALU.add)
            if i < GPSIMD_CENTRED_UNITS:
                h_part = passing("h_part", n)
                nc.scalar.activation(h_part[:], window[:, lo:hi], ACT.Copy, scale=(1.0 - M) / KAPPA)
                nc.gpsimd.tensor_tensor(centred[:], h_part[:], minus[:], ALU.add)
            else:
                nc.vector.scalar_tensor_tensor(
                    centred[:], h_sums[t][:, lo:hi], H_SCALE * (1.0 - M), minus[:], ALU.mult, ALU.add
                )
            if by_transposes:
                diff, even, total = bank(5, "diff"), bank(6, "even"), bank(7, "total")
                turn_and_add(diff, [b, a], n)
                nc.scalar.activation(diff2[:], diff[:, :n], ACT.Square, scale=DIFF_SCALE)
                turn_and_add(even, [minus, window[:, lo:hi]], n)
                nc.scalar.activation(even2[:], even[:, :n], ACT.Square, scale=EVEN_SCALE)
                turn_and_add(total, [even2, diff2], n)
            else:
                even, total = passing("even", n), passing("total", n)
                nc.vector.scalar_tensor_tensor(
                    even[:], h_sums[t][:, lo:hi], H_SCALE * KAPPA, minus[:], ALU.mult, ALU.add
                )
                nc.scalar.activation(even2[:], even[:], ACT.Square, scale=EVEN_SCALE)
                nc.scalar.activation(diff2[:], plus[:], ACT.Square, scale=DIFF_SCALE)
                nc.vector.tensor_tensor(total[:], even2[:], diff2[:], ALU.add)
            nc.scalar.activation(root[:], total[:, :n], ACT.Abs_reciprocal_sqrt, bias=0.25)
            nc.vector.tensor_tensor(result[:, t, lo:hi], centred[:], root[:], ALU.mult)
            nc.sync.dma_start(out_rows[:, t, lo:hi], result[:, t, lo:hi])
            if t == SLOTS - 1:
                out_bf16 = passing("out_bf16", n * SLOTS, BF16)
                pairs = n // 4
                nc.scalar.copy(interleaved(out_bf16)[:, :pairs], column_pairs(result[:, :, lo:hi])[:, :pairs])
                nc.vector.tensor_copy(interleaved(out_bf16)[:, pairs:], column_pairs(result[:, :, lo:hi])[:, pairs:])
                nc.vector.quantize_mx(out_codes[:, lo:hi].bitcast(FP8X4), out_scales[:, lo:hi], out_bf16[:])
                nc.sync.dma_start(words_of(out_1)[:, lo:hi], out_codes[:, lo:hi])
        for q in range(4):
            (nc.sync, nc.scalar)[q % 2].dma_start(
                out_2[0].bitcast(I32)[4 * q : 4 * q + 4, :], out_scales[:].bitcast(I32)[32 * q : 32 * q + 4, :]
            )
